import numpy as np
import ml_dtypes


def mxq(x, axis, fmt="e4m3"):
    dtype, down = {"e4m3": (ml_dtypes.float8_e4m3fn, 7), "e5m2": (ml_dtypes.float8_e5m2, 14)}[fmt]
    v = np.moveaxis(np.asarray(x, np.float32).astype(ml_dtypes.bfloat16).astype(np.float64), axis, -1)
    blocks = v.reshape(v.shape[:-1] + (-1, 32))
    amax = np.abs(blocks).max(-1, keepdims=True)
    byte = np.maximum(np.where(amax > 0, np.frexp(amax)[1] - 1 + 127, 0) - down, 1)
    scale = np.exp2(byte - 127.0)
    codes = (blocks / scale).astype(np.float32).astype(dtype).astype(np.float64)
    return np.moveaxis((codes * scale).reshape(v.shape), -1, axis)


WIDE = False


def mx_kscale(k):
    if not WIDE:
        return np.ones(k)
    levels = np.array([10, -10, 5, -5, 0])
    if k % 512:
        return np.exp2(np.random.permutation(np.resize(levels, k // 32))).repeat(32)
    a = np.empty((k // 512, 16))
    for p in range(k // 512):
        a[p, :8] = np.random.permutation(np.resize(levels, 8))
        for g in range(8):
            far = levels[np.abs(levels - a[p, g]) >= 10]
            a[p, g + 8] = far[np.random.randint(len(far))]
    return np.exp2(a.ravel()).repeat(32)


def f64(x):
    return np.asarray(x).astype(np.float64)


def striped(idx):
    return np.tile(idx.reshape(-1, 16).T, (8, 1)).astype(np.uint16)


def unstriped(offs):
    return offs[:16].T.reshape(-1).astype(np.int64)


def striped8(idx):
    return np.concatenate([x.reshape(-1, 16).T for x in idx]).astype(np.uint16)


def runs(offs, k):
    lists = np.stack([offs[16 * r : 16 * r + 16].T.reshape(-1) for r in range(8)]).astype(np.int64)
    return lists[np.arange(k) % 512 // 64]


def pack_weight(w):
    k, n = w.shape
    w = f64(np.asarray(w, np.float32).astype(ml_dtypes.bfloat16)).reshape(k // 32, 32, n)
    amax = np.abs(w).max(1)
    byte = np.clip(np.where(amax > 0, np.frexp(amax)[1] - 1 + 127 - 7, 1), 1, 254)
    scaled = (w * np.exp2(127.0 - byte)[:, None, :]).reshape(k, n).astype(np.float32)
    words = np.ascontiguousarray(scaled.reshape(k // 512, 128, 4, n).transpose(0, 1, 3, 2)).astype(ml_dtypes.float8_e4m3fn).view(np.uint8)
    return words, np.ascontiguousarray(byte.astype(np.uint8).reshape(k // 512, 16, n))


def unpack_weight(words, scales):
    g, p, n, _ = words.shape
    vals = np.ascontiguousarray(words).view(ml_dtypes.float8_e4m3fn).astype(np.float64) * np.repeat(np.exp2(scales.astype(np.float64) - 127.0), 8, axis=1)[..., None]
    return vals.transpose(0, 1, 3, 2).reshape(g * 512, n)


E2M1 = np.array([0.0, 0.5, 1.0, 1.5, 2.0, 3.0, 4.0, 6.0, -0.0, -0.5, -1.0, -1.5, -2.0, -3.0, -4.0, -6.0])


def pack_fp4(w):
    k, n = w.shape
    w = f64(np.asarray(w, np.float32).astype(ml_dtypes.bfloat16)).reshape(k // 32, 32, n)
    amax = np.abs(w).max(1)
    mant, ex = np.frexp(amax / 6.0)
    byte = np.clip(np.where(amax > 0, np.where(mant > 0.5, ex, ex - 1) + 127, 1), 1, 254)
    scaled = (w * np.exp2(127.0 - byte)[:, None, :]).reshape(k, n).astype(np.float32)
    c = np.ascontiguousarray(scaled.reshape(k // 512, 128, 4, n).transpose(0, 1, 3, 2)).astype(ml_dtypes.float4_e2m1fn).view(np.uint8) & 0xF
    words = (c[..., 0::2] | (c[..., 1::2] << 4)).reshape(k // 512, 128, 2 * n)
    return np.ascontiguousarray(words), np.ascontiguousarray(byte.astype(np.uint8).reshape(k // 512, 16, n))


def unpack_fp4(words, scales):
    g, _, n = scales.shape
    words = np.ascontiguousarray(words).reshape(g, 128, n, 2)
    nib = np.empty((g, 128, n, 4), np.uint8)
    nib[..., 0::2] = words & 0xF
    nib[..., 1::2] = words >> 4
    vals = E2M1[nib] * np.repeat(np.exp2(scales.astype(np.float64) - 127.0), 8, axis=1)[..., None]
    return vals.transpose(0, 1, 3, 2).reshape(g * 512, n)


def planes(y):
    n, m = y.shape
    v = y.astype(np.float32).astype(ml_dtypes.bfloat16).astype(np.float64).reshape(n // 32, 32, m)
    top = np.abs(v).max(1)
    byte = np.clip(np.where(top > 0, np.frexp(top)[1] - 1 + 127 - 7, 1), 1, 254)
    codes = (v * np.exp2(127.0 - byte)[:, None, :]).reshape(n, m).astype(np.float32).astype(ml_dtypes.float8_e4m3fn).view(np.uint8)
    words = codes.reshape(n // 512, 128, 4, m).transpose(0, 1, 3, 2)
    return np.ascontiguousarray(words), np.ascontiguousarray(byte.astype(np.uint8).reshape(n // 512, 16, m))


K, T, S, N, H = 512, 2048, 512, 512, 512
P = 2 ** 7


def setup_inputs():
    n = np.random.standard_normal
    s = mx_kscale(K)[:, None]
    u = mx_kscale(H)
    packed_xT = pack_weight(n((K, T)) * s)
    packed_w2 = pack_fp4(n((H, N)) / np.sqrt(3 * H) / u[:, None])
    packed_w3 = pack_fp4(n((H, N)) / np.sqrt(3 * H) / u[:, None])
    packed_w4 = pack_fp4(n((H, N)) / np.sqrt(3 * H) / u[:, None])
    return {
        "x_words": packed_xT[0],
        "x_scales": packed_xT[1],
        "w1": (n((K, H)) / np.sqrt(K) / s * u).astype(np.float32),
        "ga": np.tile(np.random.uniform(0.2, 1.0, S), (P, 1)).astype(np.float32),
        "gb": np.tile(np.random.uniform(0.2, 1.0, S), (P, 1)).astype(np.float32),
        "w2_words": packed_w2[0],
        "w2_scales": packed_w2[1],
        "w3_words": packed_w3[0],
        "w3_scales": packed_w3[1],
        "w4_words": packed_w4[0],
        "w4_scales": packed_w4[1],
        "offs": striped(np.random.permutation(T)[:S]),
        "p1": striped8(np.stack([np.random.permutation(S) for _ in range(8)])),
        "p2": striped8(np.stack([np.random.permutation(S) for _ in range(8)])),
    }


def reference(x_words, x_scales, w1, ga, gb, w2_words, w2_scales, w3_words, w3_scales, w4_words, w4_scales, offs, p1, p2):
    xq = unpack_weight(x_words, x_scales)[:, unstriped(offs)]
    y = mxq(f64(w1), 0, "e4m3").T @ xq
    h = f64(ga)[:1] * (y[np.arange(H)[:, None], runs(p1, H)]) + f64(gb)[:1] * (y[np.arange(H)[:, None], runs(p2, H)])
    z = 2.0 * (f64(ga)[:1] * (h[np.arange(H)[:, None], runs(p1, H)]) + f64(gb)[:1] * (h[np.arange(H)[:, None], runs(p2, H)])) - y
    out_0 = unpack_fp4(w2_words, w2_scales).T @ mxq(y, 0, "e4m3") + unpack_fp4(w3_words, w3_scales).T @ mxq(h, 0, "e4m3") + unpack_fp4(w4_words, w4_scales).T @ mxq(z, 0, "e4m3")
    return (out_0,) + planes(out_0)

@@ -1,0 +1,170 @@
+from contextlib import ExitStack
+
+import concourse.mybir as mybir
+from concourse.masks import make_identity
+
+K, T, S, H, N = 512, 2048, 512, 512, 512
+FLOPS = 4 * 2 * 512 * 512 * 512
+
+F32 = mybir.dt.float32
+BF16 = mybir.dt.bfloat16
+I32 = mybir.dt.int32
+U32 = mybir.dt.uint32
+U16 = mybir.dt.uint16
+U8 = mybir.dt.uint8
+FP8X4 = mybir.dt.float8_e4m3fn_x4
+FP4X4 = mybir.dt.float4_e2m1fn_x4
+MULT = mybir.AluOpType.mult
+ADD = mybir.AluOpType.add
+SUB = mybir.AluOpType.subtract
+
+P = 128
+PACK = 4
+LANES = 16
+Z_CHUNKS = ((0, 256), (256, 128), (384, 128))
+W1_VECTOR_M = 80
+
+
+def tile_picked_cheb3_none_po_kernel(
+    tc, x_words, x_scales, w1, ga, gb, w2_words, w2_scales, w3_words, w3_scales, w4_words, w4_scales,
+    offs, p1, p2, out_0, out_1, out_2,
+):
+    nc = tc.nc
+    with ExitStack() as ctx:
+        keep = ctx.enter_context(tc.tile_pool(name="keep", bufs=1))
+        ring = ctx.enter_context(tc.tile_pool(name="ring", bufs=2))
+        psum = ctx.enter_context(tc.psum_pool(name="psum", bufs=1))
+
+        offs_sb = keep.tile([P, S // LANES], U16, name="offs_sb")
+        p1_sb = keep.tile([P, S // LANES], U16, name="p1_sb")
+        p2_sb = keep.tile([P, S // LANES], U16, name="p2_sb")
+        xs_sb = keep.tile([P, T], U8, name="xs_sb", align_bytes=64)
+        xw_sb = keep.tile([P, T], U32, name="xw_sb", align_bytes=64)
+        w1_raw = keep.tile([P, PACK, H], F32, name="w1_raw", align_bytes=64)
+        gate = keep.tile([P, 2, S], F32, name="gate", align_bytes=64)
+        gate2 = keep.tile([P, 2, S], F32, name="gate2", align_bytes=64)
+        w_words = [keep.tile([P, 2 * N], U8, name="w_words%d" % a, align_bytes=64) for a in range(3)]
+        w_scales = [keep.tile([P, N], U8, name="w_scales%d" % a, align_bytes=64) for a in range(3)]
+        y_win = [keep.tile([P, 2 * S], F32, name="y_win%d" % t, align_bytes=64) for t in range(PACK)]
+        h_win = [keep.tile([P, S], F32, name="h_win%d" % t, align_bytes=64) for t in range(PACK)]
+        ident = keep.tile([P, P], F32, name="ident", align_bytes=64)
+
+        def load_scale_rows(tile, rows):
+            for q in range(4):
+                nc.sync.dma_start(tile[32 * q : 32 * q + 4, :].bitcast(I32), rows[0, 4 * q : 4 * q + 4, :].bitcast(I32))
+
+        nc.vector.memset(xs_sb[:].bitcast(I32), 0)
+        nc.sync.dma_start(offs_sb[:], offs)
+        load_scale_rows(xs_sb, x_scales)
+        nc.sync.dma_start(w1_raw[:], w1.rearrange("(p j) c -> p j c", j=PACK))
+        nc.sync.dma_start(xw_sb[:].bitcast(I32), x_words[0].rearrange("p n t -> p (n t)").bitcast(I32))
+        nc.sync.dma_start(p1_sb[:], p1)
+        nc.sync.dma_start(gate[:, 0, :], ga)
+        nc.sync.dma_start(p2_sb[:], p2)
+        nc.sync.dma_start(gate[:, 1, :], gb)
+        for a, words in enumerate((w2_words, w3_words, w4_words)):
+            nc.sync.dma_start(w_words[a][:].bitcast(I32), words[0].bitcast(I32))
+        for a, rows in enumerate((w2_scales, w3_scales, w4_scales)):
+            nc.gpsimd.memset(w_scales[a][:].bitcast(I32), 0)
+            load_scale_rows(w_scales[a], rows)
+        for t in range(PACK):
+            nc.gpsimd.memset(y_win[t][:, S:], 0.0)
+        make_identity(nc, ident[:])
+
+        xs_pick = keep.tile([P, S], U8, name="xs_pick", align_bytes=64)
+        xw_pick = keep.tile([P, S], U32, name="xw_pick", align_bytes=64)
+        nc.vector.tensor_copy(xs_pick[:], xs_sb[:].indirect(offs_sb[:]))
+
+        w1_bf = keep.tile([P, PACK * H], BF16, name="w1_bf", align_bytes=64)
+        w1_dst = w1_bf[:].rearrange("p (t m j) -> p m t j", t=PACK, j=PACK)
+        w1_src = w1_raw[:].rearrange("p j (m t) -> p m t j", t=PACK)
+        nc.vector.tensor_copy(w1_dst[:, :W1_VECTOR_M], w1_src[:, :W1_VECTOR_M])
+        nc.scalar.copy(w1_dst[:, W1_VECTOR_M:], w1_src[:, W1_VECTOR_M:])
+        w1_codes = keep.tile([P, H], U32, name="w1_codes", align_bytes=64)
+        w1_scales = keep.tile([P, H], U8, name="w1_scales", align_bytes=64)
+        nc.vector.quantize_mx(out=w1_codes[:].bitcast(FP8X4), scales=w1_scales[:], in_=w1_bf[:])
+        nc.vector.tensor_copy(xw_pick[:], xw_sb[:].indirect(offs_sb[:]))
+        nc.scalar.mul(gate2[:], gate[:], 2.0)
+
+        y_cat = keep.tile([P, PACK, S], F32, name="y_cat", align_bytes=64)
+        y_banks = []
+        for t in range(PACK):
+            bank = psum.tile([P, S], F32, name="y_bank%d" % t, tag="acc%d" % t)
+            cols = slice(t * P, (t + 1) * P)
+            nc.tensor.matmul_mx(out=bank[:], lhsT=w1_codes[:, cols].bitcast(FP8X4), lhsT_scale=w1_scales[:, cols],
+                                rhs=xw_pick[:].bitcast(FP8X4), rhs_scale=xs_pick[:], start=True, stop=True)
+            nc.scalar.copy(y_win[t][:, :S], bank[:])
+            y_banks.append(bank)
+        for t in range(PACK):
+            nc.scalar.copy(y_cat[:, t, :], y_banks[t][:])
+        y_bf = keep.tile([P, PACK * S], BF16, name="y_bf", align_bytes=64)
+        nc.scalar.copy(y_bf[:].rearrange("p (c i t) -> p c t i", i=4, t=PACK),
+                       y_cat[:].rearrange("p t (c i) -> p c t i", i=4))
+
+        h_bf = keep.tile([P, PACK * S], BF16, name="h_bf", align_bytes=64)
+        for t in range(PACK):
+            first = ring.tile([P, S], F32, name="first", align_bytes=64)
+            second = ring.tile([P, S], F32, name="second", align_bytes=64)
+            nc.vector.tensor_tensor(first[:], y_win[t][:].indirect(p1_sb[:]), gate[:, 0, :], MULT)
+            nc.vector.tensor_tensor(second[:], y_win[t][:].indirect(p2_sb[:]), gate[:, 1, :], MULT)
+            nc.vector.tensor_tensor(h_win[t][:], first[:], second[:], ADD)
+            nc.scalar.copy(h_bf[:].rearrange("p (j t) -> p t j", t=PACK)[:, t, :], h_win[t][:])
+
+        def quantize(name, values, width):
+            codes = keep.tile([P, width], U32, name=name + "_codes", align_bytes=64)
+            scales = keep.tile([P, width], U8, name=name + "_scales", align_bytes=64)
+            nc.vector.quantize_mx(out=codes[:].bitcast(FP8X4), scales=scales[:], in_=values)
+            return codes, scales
+
+        out_banks = [psum.tile([P, N], F32, name="out_bank%d" % c, tag="acc%d" % c) for c in range(S // P)]
+
+        def product(a, codes, scales, c, col0):
+            cols = slice(col0, col0 + P)
+            nc.tensor.matmul_mx(out=out_banks[c][:], lhsT=codes[:, cols].bitcast(FP8X4), lhsT_scale=scales[:, cols],
+                                rhs=w_words[a][:].bitcast(FP4X4), rhs_scale=w_scales[a][:], start=(a == 0), stop=(a == 2))
+
+        y_codes, y_scales = quantize("y", y_bf[:], S)
+        for c in range(S // P):
+            product(0, y_codes, y_scales, c, c * P)
+        h_codes, h_scales = quantize("h", h_bf[:], S)
+        for c in range(S // P):
+            product(1, h_codes, h_scales, c, c * P)
+
+        o_codes = keep.tile([P, S], U32, name="o_codes", align_bytes=64)
+        o_scales = keep.tile([P, S], U8, name="o_scales", align_bytes=64)
+        out_rows = out_0.rearrange("(p t) j -> p t j", t=PACK)
+        out_words = out_1[0].rearrange("p n t -> p (n t)").bitcast(I32)
+        for j0, width in Z_CHUNKS:
+            cols = slice(j0, j0 + width)
+            entries = slice(j0 // LANES, (j0 + width) // LANES)
+            za = keep.tile([P, PACK, width], F32, name="za%d" % j0, align_bytes=64)
+            zb = keep.tile([P, PACK, width], F32, name="zb%d" % j0, align_bytes=64)
+            zs = keep.tile([P, PACK, width], F32, name="zs%d" % j0, align_bytes=64)
+            z_bf = keep.tile([P, PACK * width], BF16, name="z_bf%d" % j0, align_bytes=64)
+            for t in range(PACK):
+                nc.vector.tensor_tensor(za[:, t, :], h_win[t][:].indirect(p1_sb[:, entries]), gate2[:, 0, cols], MULT)
+            nc.vector.tensor_tensor(zs[:], za[:], y_cat[:, :, cols], SUB)
+            for t in range(PACK):
+                nc.vector.tensor_tensor(zb[:, t, :], h_win[t][:].indirect(p2_sb[:, entries]), gate2[:, 1, cols], MULT)
+            nc.vector.tensor_tensor(z_bf[:].rearrange("p (c i t) -> p c t i", i=4, t=PACK),
+                                    zs[:].rearrange("p t (c i) -> p c t i", i=4),
+                                    zb[:].rearrange("p t (c i) -> p c t i", i=4), ADD)
+            z_codes, z_scales = quantize("z%d" % j0, z_bf[:], width)
+            for c in range(j0 // P, (j0 + width) // P):
+                product(2, z_codes, z_scales, c, c * P - j0)
+                block = slice(c * P, (c + 1) * P)
+                turned = ring.tile([P, PACK, P], F32, name="turned", align_bytes=64)
+                nc.scalar.copy(turned[:], out_banks[c][:].rearrange("j (p t) -> j t p", t=PACK))
+                back = psum.tile([P, PACK, P], F32, name="back", tag="back%d" % (c % 2))
+                for t in range(PACK):
+                    nc.tensor.transpose(back[:, t, :], turned[:, t, :], ident[:])
+                o_bf = ring.tile([P, PACK * P], BF16, name="o_bf", align_bytes=64)
+                nc.scalar.copy(o_bf[:].rearrange("p (j t) -> p j t", t=PACK), back[:].rearrange("p t j -> p j t"))
+                o_f32 = ring.tile([P, PACK, P], F32, name="o_f32", align_bytes=64)
+                nc.scalar.copy(o_f32[:], back[:])
+                nc.sync.dma_start(out_rows[:, :, block], o_f32[:])
+                nc.vector.quantize_mx(out=o_codes[:, block].bitcast(FP8X4), scales=o_scales[:, block], in_=o_bf[:])
+                nc.sync.dma_start(out_words[:, block], o_codes[:, block].bitcast(I32))
+        for q in range(4):
+            queue = nc.sync if q % 2 == 0 else nc.scalar
+            queue.dma_start(out_2[0, 4 * q : 4 * q + 4, :].bitcast(I32), o_scales[32 * q : 32 * q + 4, :].bitcast(I32))

@@ -16,13 +16,11 @@ FP8X4 = mybir.dt.float8_e4m3fn_x4
 FP4X4 = mybir.dt.float4_e2m1fn_x4
 MULT = mybir.AluOpType.mult
 ADD = mybir.AluOpType.add
-SUB = mybir.AluOpType.subtract
 
 P = 128
 PACK = 4
 LANES = 16
-Z_CHUNKS = ((0, 256), (256, 128), (384, 128))
-W1_VECTOR_M = 80
+W1_VECTOR_M = 56
 
 
 def tile_picked_cheb3_none_po_kernel(
@@ -32,7 +30,7 @@ def tile_picked_cheb3_none_po_kernel(
     nc = tc.nc
     with ExitStack() as ctx:
         keep = ctx.enter_context(tc.tile_pool(name="keep", bufs=1))
-        ring = ctx.enter_context(tc.tile_pool(name="ring", bufs=2))
+        ring = ctx.enter_context(tc.tile_pool(name="ring", bufs=4))
         psum = ctx.enter_context(tc.psum_pool(name="psum", bufs=1))
 
         offs_sb = keep.tile([P, S // LANES], U16, name="offs_sb")
@@ -42,7 +40,6 @@ def tile_picked_cheb3_none_po_kernel(
         xw_sb = keep.tile([P, T], U32, name="xw_sb", align_bytes=64)
         w1_raw = keep.tile([P, PACK, H], F32, name="w1_raw", align_bytes=64)
         gate = keep.tile([P, 2, S], F32, name="gate", align_bytes=64)
-        gate2 = keep.tile([P, 2, S], F32, name="gate2", align_bytes=64)
         w_words = [keep.tile([P, 2 * N], U8, name="w_words%d" % a, align_bytes=64) for a in range(3)]
         w_scales = [keep.tile([P, N], U8, name="w_scales%d" % a, align_bytes=64) for a in range(3)]
         y_win = [keep.tile([P, 2 * S], F32, name="y_win%d" % t, align_bytes=64) for t in range(PACK)]
@@ -53,10 +50,10 @@ def tile_picked_cheb3_none_po_kernel(
             for q in range(4):
                 nc.sync.dma_start(tile[32 * q : 32 * q + 4, :].bitcast(I32), rows[0, 4 * q : 4 * q + 4, :].bitcast(I32))
 
-        nc.vector.memset(xs_sb[:].bitcast(I32), 0)
+        nc.gpsimd.memset(xs_sb[:].bitcast(I32), 0)
+        nc.sync.dma_start(w1_raw[:], w1.rearrange("(p j) c -> p j c", j=PACK))
         nc.sync.dma_start(offs_sb[:], offs)
         load_scale_rows(xs_sb, x_scales)
-        nc.sync.dma_start(w1_raw[:], w1.rearrange("(p j) c -> p j c", j=PACK))
         nc.sync.dma_start(xw_sb[:].bitcast(I32), x_words[0].rearrange("p n t -> p (n t)").bitcast(I32))
         nc.sync.dma_start(p1_sb[:], p1)
         nc.sync.dma_start(gate[:, 0, :], ga)
@@ -71,44 +68,34 @@ def tile_picked_cheb3_none_po_kernel(
             nc.gpsimd.memset(y_win[t][:, S:], 0.0)
         make_identity(nc, ident[:])
 
-        xs_pick = keep.tile([P, S], U8, name="xs_pick", align_bytes=64)
-        xw_pick = keep.tile([P, S], U32, name="xw_pick", align_bytes=64)
-        nc.vector.tensor_copy(xs_pick[:], xs_sb[:].indirect(offs_sb[:]))
-
         w1_bf = keep.tile([P, PACK * H], BF16, name="w1_bf", align_bytes=64)
         w1_dst = w1_bf[:].rearrange("p (t m j) -> p m t j", t=PACK, j=PACK)
         w1_src = w1_raw[:].rearrange("p j (m t) -> p m t j", t=PACK)
         nc.vector.tensor_copy(w1_dst[:, :W1_VECTOR_M], w1_src[:, :W1_VECTOR_M])
         nc.scalar.copy(w1_dst[:, W1_VECTOR_M:], w1_src[:, W1_VECTOR_M:])
+        xs_pick = keep.tile([P, S], U8, name="xs_pick", align_bytes=64)
+        nc.vector.tensor_copy(xs_pick[:], xs_sb[:].indirect(offs_sb[:]))
         w1_codes = keep.tile([P, H], U32, name="w1_codes", align_bytes=64)
         w1_scales = keep.tile([P, H], U8, name="w1_scales", align_bytes=64)
         nc.vector.quantize_mx(out=w1_codes[:].bitcast(FP8X4), scales=w1_scales[:], in_=w1_bf[:])
-        nc.vector.tensor_copy(xw_pick[:], xw_sb[:].indirect(offs_sb[:]))
-        nc.scalar.mul(gate2[:], gate[:], 2.0)
+        half = S // 2
+        xw_pick = []
+        for u in range(2):
+            picked = keep.tile([P, half], U32, name="xw_pick%d" % u, align_bytes=64)
+            entries = slice(u * half // LANES, (u + 1) * half // LANES)
+            nc.vector.tensor_copy(picked[:], xw_sb[:].indirect(offs_sb[:, entries]))
+            xw_pick.append(picked)
 
-        y_cat = keep.tile([P, PACK, S], F32, name="y_cat", align_bytes=64)
-        y_banks = []
+        blocks = [slice(c * P, (c + 1) * P) for c in range(S // P)]
+        y_banks = [psum.tile([P, PACK, P], F32, name="y_bank%d" % c, tag="acc%d" % c) for c in range(S // P)]
         for t in range(PACK):
-            bank = psum.tile([P, S], F32, name="y_bank%d" % t, tag="acc%d" % t)
-            cols = slice(t * P, (t + 1) * P)
-            nc.tensor.matmul_mx(out=bank[:], lhsT=w1_codes[:, cols].bitcast(FP8X4), lhsT_scale=w1_scales[:, cols],
-                                rhs=xw_pick[:].bitcast(FP8X4), rhs_scale=xs_pick[:], start=True, stop=True)
-            nc.scalar.copy(y_win[t][:, :S], bank[:])
-            y_banks.append(bank)
-        for t in range(PACK):
-            nc.scalar.copy(y_cat[:, t, :], y_banks[t][:])
-        y_bf = keep.tile([P, PACK * S], BF16, name="y_bf", align_bytes=64)
-        nc.scalar.copy(y_bf[:].rearrange("p (c i t) -> p c t i", i=4, t=PACK),
-                       y_cat[:].rearrange("p t (c i) -> p c t i", i=4))
-
-        h_bf = keep.tile([P, PACK * S], BF16, name="h_bf", align_bytes=64)
-        for t in range(PACK):
-            first = ring.tile([P, S], F32, name="first", align_bytes=64)
-            second = ring.tile([P, S], F32, name="second", align_bytes=64)
-            nc.vector.tensor_tensor(first[:], y_win[t][:].indirect(p1_sb[:]), gate[:, 0, :], MULT)
-            nc.vector.tensor_tensor(second[:], y_win[t][:].indirect(p2_sb[:]), gate[:, 1, :], MULT)
-            nc.vector.tensor_tensor(h_win[t][:], first[:], second[:], ADD)
-            nc.scalar.copy(h_bf[:].rearrange("p (j t) -> p t j", t=PACK)[:, t, :], h_win[t][:])
+            for c, block in enumerate(blocks):
+                nc.tensor.matmul_mx(out=y_banks[c][:, t, :], lhsT=w1_codes[:, blocks[t]].bitcast(FP8X4),
+                                    lhsT_scale=w1_scales[:, blocks[t]],
+                                    rhs=xw_pick[c // 2][:, blocks[c % 2]].bitcast(FP8X4), rhs_scale=xs_pick[:, block],
+                                    start=True, stop=True)
+                nc.scalar.mul(y_win[t][:, block], y_banks[c][:, t, :], -1.0)
+        y_bf = keep.tile([P, S, PACK], BF16, name="y_bf", align_bytes=64)
 
         def quantize(name, values, width):
             codes = keep.tile([P, width], U32, name=name + "_codes", align_bytes=64)
@@ -118,53 +105,153 @@ def tile_picked_cheb3_none_po_kernel(
 
         out_banks = [psum.tile([P, N], F32, name="out_bank%d" % c, tag="acc%d" % c) for c in range(S // P)]
 
-        def product(a, codes, scales, c, col0):
-            cols = slice(col0, col0 + P)
-            nc.tensor.matmul_mx(out=out_banks[c][:], lhsT=codes[:, cols].bitcast(FP8X4), lhsT_scale=scales[:, cols],
+        def product(a, codes, scales, c):
+            nc.tensor.matmul_mx(out=out_banks[c][:], lhsT=codes.bitcast(FP8X4), lhsT_scale=scales,
                                 rhs=w_words[a][:].bitcast(FP4X4), rhs_scale=w_scales[a][:], start=(a == 0), stop=(a == 2))
 
-        y_codes, y_scales = quantize("y", y_bf[:], S)
-        for c in range(S // P):
-            product(0, y_codes, y_scales, c, c * P)
-        h_codes, h_scales = quantize("h", h_bf[:], S)
-        for c in range(S // P):
-            product(1, h_codes, h_scales, c, c * P)
+        def add_turned(bank, terms):
+            for i, (slot, term) in enumerate(terms):
+                nc.tensor.matmul(bank[:, slot, :], lhsT=term, rhs=ident[:], is_transpose=True,
+                                 start=(i == 0), stop=(i == len(terms) - 1))
 
-        o_codes = keep.tile([P, S], U32, name="o_codes", align_bytes=64)
+        def pairs_back(sorted_bf, dst, tag, copy):
+            pairs = psum.tile([P, 2, P], F32, name="pairs", tag=tag)
+            for u in range(2):
+                nc.tensor.transpose(pairs[:, u, :], sorted_bf[:].bitcast(F32)[:, blocks[u]], ident[:])
+            copy(dst.bitcast(F32).rearrange("p (j u) -> p j u", u=2), pairs[:].rearrange("p u j -> p j u"))
+
+        h_nodes = keep.tile([P, PACK, S // P, P], F32, name="h_nodes", align_bytes=64)
+        for t in range(PACK):
+            first = ring.tile([P, S], F32, name="first", align_bytes=64)
+            second = ring.tile([P, S], F32, name="second", align_bytes=64)
+            nc.vector.tensor_tensor(first[:], y_win[t][:].indirect(p1_sb[:]), gate[:, 0, :], MULT)
+            nc.vector.tensor_tensor(second[:], y_win[t][:].indirect(p2_sb[:]), gate[:, 1, :], MULT)
+            summed = psum.tile([P, S // P, P], F32, name="summed", tag="a%d" % (t % 2))
+            add_turned(summed, [(c, term[:, block]) for term in (first, second) for c, block in enumerate(blocks)])
+            nc.scalar.mul(h_nodes[:, t], summed[:], -1.0)
+            h_back = psum.tile([P, S // P, P], F32, name="h_back", tag="b%d" % (t % 2))
+            for c in range(S // P):
+                nc.tensor.transpose(h_back[:, c, :], h_nodes[:, t, c, :], ident[:])
+            nc.scalar.mul(h_win[t][:], h_back[:].rearrange("p c j -> p (c j)"), 2.0)
+            nc.scalar.copy(y_bf[:, blocks[t], :], y_banks[t][:].rearrange("p t j -> p j t"))
+        y_codes, y_scales = quantize("y", y_bf[:].rearrange("p j t -> p (j t)"), S)
+        for c, block in enumerate(blocks):
+            product(0, y_codes[:, block], y_scales[:, block], c)
+
+        h_bf = keep.tile([P, S * PACK], BF16, name="h_bf", tag="h_bf_slot", align_bytes=64)
+        for c in range(S // P):
+            h_sorted = ring.tile([P, PACK * P], BF16, name="h_sorted", align_bytes=64)
+            nc.scalar.copy(h_sorted[:].rearrange("j (u p e) -> j u p e", u=2, e=2),
+                           h_nodes[:, :, c, :].rearrange("j (u e) p -> j u p e", u=2))
+            pairs_back(h_sorted, h_bf[:, c * PACK * P : (c + 1) * PACK * P], "b%d" % (c % 2), nc.scalar.copy)
+
         o_scales = keep.tile([P, S], U8, name="o_scales", align_bytes=64)
         out_rows = out_0.rearrange("(p t) j -> p t j", t=PACK)
         out_words = out_1[0].rearrange("p n t -> p (n t)").bitcast(I32)
-        for j0, width in Z_CHUNKS:
-            cols = slice(j0, j0 + width)
+
+        def neighbours(a, j0, width, tag):
             entries = slice(j0 // LANES, (j0 + width) // LANES)
-            za = keep.tile([P, PACK, width], F32, name="za%d" % j0, align_bytes=64)
-            zb = keep.tile([P, PACK, width], F32, name="zb%d" % j0, align_bytes=64)
-            zs = keep.tile([P, PACK, width], F32, name="zs%d" % j0, align_bytes=64)
-            z_bf = keep.tile([P, PACK * width], BF16, name="z_bf%d" % j0, align_bytes=64)
+            picked = keep.tile([P, PACK, width], F32, name="picked%d_%d" % (a, j0), tag=tag, align_bytes=64)
             for t in range(PACK):
-                nc.vector.tensor_tensor(za[:, t, :], h_win[t][:].indirect(p1_sb[:, entries]), gate2[:, 0, cols], MULT)
-            nc.vector.tensor_tensor(zs[:], za[:], y_cat[:, :, cols], SUB)
+                nc.vector.tensor_tensor(picked[:, t, :], h_win[t][:].indirect((p1_sb, p2_sb)[a][:, entries]),
+                                        gate[:, a, j0 : j0 + width], MULT)
+            return picked
+
+        def neighbours_by_row(j0, width):
+            entries = slice(j0 // LANES, (j0 + width) // LANES)
+            both = [keep.tile([P, PACK, width], F32, name="both%d_%d" % (a, j0), align_bytes=64) for a in range(2)]
             for t in range(PACK):
-                nc.vector.tensor_tensor(zb[:, t, :], h_win[t][:].indirect(p2_sb[:, entries]), gate2[:, 1, cols], MULT)
+                for a in range(2):
+                    nc.vector.tensor_tensor(both[a][:, t, :], h_win[t][:].indirect((p1_sb, p2_sb)[a][:, entries]),
+                                            gate[:, a, j0 : j0 + width], MULT)
+            return both
+
+        def sum_on_tensor(c, za, zb, local, tag):
+            zt = psum.tile([P, PACK, P], F32, name="zt", tag="a%d" % (c % 2))
+            terms = [(t, y_win[t][:, blocks[c]]) for t in range(PACK)]
+            for t in range(PACK):
+                terms = terms + [(t, za[:, t, local]), (t, zb[:, t, local])]
+            add_turned(zt, terms)
+            z_sorted = ring.tile([P, PACK * P], BF16, name="z_sorted", align_bytes=64)
+            nc.scalar.copy(z_sorted[:].rearrange("j (u p e) -> j u p e", u=2, e=2),
+                           zt[:].rearrange("j (u e) p -> j u p e", u=2))
+            z_bf = keep.tile([P, PACK * P], BF16, name="z_bf%d" % c, tag=tag, align_bytes=64)
+            pairs_back(z_sorted, z_bf[:], "b0", nc.scalar.copy)
+            return z_bf
+
+        def sum_on_vector(c, za, zb):
+            zs = keep.tile([P, PACK, P], F32, name="zs", tag="z2_slot", align_bytes=64)
+            for t in range(PACK):
+                nc.vector.tensor_tensor(zs[:, t, :], za[:, t, :], y_win[t][:, blocks[c]], ADD)
+            z_bf = ring.tile([P, PACK * P], BF16, name="z_bf", align_bytes=64)
             nc.vector.tensor_tensor(z_bf[:].rearrange("p (c i t) -> p c t i", i=4, t=PACK),
                                     zs[:].rearrange("p t (c i) -> p c t i", i=4),
                                     zb[:].rearrange("p t (c i) -> p c t i", i=4), ADD)
-            z_codes, z_scales = quantize("z%d" % j0, z_bf[:], width)
-            for c in range(j0 // P, (j0 + width) // P):
-                product(2, z_codes, z_scales, c, c * P - j0)
-                block = slice(c * P, (c + 1) * P)
-                turned = ring.tile([P, PACK, P], F32, name="turned", align_bytes=64)
-                nc.scalar.copy(turned[:], out_banks[c][:].rearrange("j (p t) -> j t p", t=PACK))
-                back = psum.tile([P, PACK, P], F32, name="back", tag="back%d" % (c % 2))
-                for t in range(PACK):
-                    nc.tensor.transpose(back[:, t, :], turned[:, t, :], ident[:])
-                o_bf = ring.tile([P, PACK * P], BF16, name="o_bf", align_bytes=64)
-                nc.scalar.copy(o_bf[:].rearrange("p (j t) -> p j t", t=PACK), back[:].rearrange("p t j -> p j t"))
-                o_f32 = ring.tile([P, PACK, P], F32, name="o_f32", align_bytes=64)
-                nc.scalar.copy(o_f32[:], back[:])
-                nc.sync.dma_start(out_rows[:, :, block], o_f32[:])
-                nc.vector.quantize_mx(out=o_codes[:, block].bitcast(FP8X4), scales=o_scales[:, block], in_=o_bf[:])
-                nc.sync.dma_start(out_words[:, block], o_codes[:, block].bitcast(I32))
+            return z_bf
+
+        def last_product(c, z_bf):
+            z_codes, z_scales = quantize("z%d" % c, z_bf[:], P)
+            product(2, z_codes[:], z_scales[:], c)
+
+        def turn_back(c):
+            turned = ring.tile([P, PACK, P], F32, name="turned", align_bytes=64)
+            nc.scalar.copy(turned[:], out_banks[c][:].rearrange("j (p t) -> j t p", t=PACK))
+            back = psum.tile([P, PACK, P], F32, name="back", tag=("b1", "a1")[c % 2])
+            for t in range(PACK):
+                nc.tensor.transpose(back[:, t, :], turned[:, t, :], ident[:])
+            return turned, back
+
+        def store_rows(c, back):
+            o_f32 = ring.tile([P, PACK, P], F32, name="o_f32", align_bytes=64)
+            nc.scalar.copy(o_f32[:], back[:])
+            nc.sync.dma_start(out_rows[:, :, blocks[c]], o_f32[:])
+
+        def finish_on_scalar(c):
+            turned, back = turn_back(c)
+            o_bf = ring.tile([P, PACK * P], BF16, name="o_bf", align_bytes=64)
+            nc.scalar.copy(o_bf[:].rearrange("p (j t) -> p j t", t=PACK), back[:].rearrange("p t j -> p j t"))
+            store_rows(c, back)
+            return o_bf
+
+        def finish_on_both(c):
+            turned, back = turn_back(c)
+            o_sorted = ring.tile([P, PACK * P], BF16, name="o_sorted", align_bytes=64)
+            nc.vector.tensor_copy(o_sorted[:].rearrange("j (u p e) -> j u p e", u=2, e=2),
+                                  turned[:].rearrange("j (u e) p -> j u p e", u=2))
+            o_bf = ring.tile([P, PACK * P], BF16, name="o_bf", align_bytes=64)
+            pairs_back(o_sorted, o_bf[:], "a0", nc.vector.tensor_copy)
+            store_rows(c, back)
+            return o_bf
+
+        def hand_on(c, o_bf):
+            nc.vector.quantize_mx(out=o_codes[:, blocks[c]].bitcast(FP8X4), scales=o_scales[:, blocks[c]], in_=o_bf[:])
+            nc.sync.dma_start(out_words[:, blocks[c]], o_codes[:, blocks[c]].bitcast(I32))
+
+        za01, zb01 = neighbours_by_row(0, 2 * P)
+        z_bf0 = sum_on_tensor(0, za01, zb01, blocks[0], "z0_slot")
+        z_bf1 = sum_on_tensor(1, za01, zb01, blocks[1], "z1_slot")
+        za2 = neighbours(0, 2 * P, P, "za2")
+        h_codes, h_scales = quantize("h", h_bf[:], S)
+        for c, block in enumerate(blocks):
+            product(1, h_codes[:, block], h_scales[:, block], c)
+        zb2 = neighbours(1, 2 * P, P, "h_bf_slot")
+        last_product(0, z_bf0)
+        last_product(1, z_bf1)
+        z_bf2 = sum_on_tensor(2, za2, zb2, blocks[0], "z2_slot")
+        o_bf0 = finish_on_scalar(0)
+        o_bf1 = finish_on_scalar(1)
+        za3 = neighbours(0, 3 * P, P, "z0_slot")
+        zb3 = neighbours(1, 3 * P, P, "z1_slot")
+        last_product(2, z_bf2)
+        o_bf2 = finish_on_scalar(2)
+        z_bf3 = sum_on_vector(3, za3, zb3)
+        last_product(3, z_bf3)
+        o_codes = keep.tile([P, S], U32, name="o_codes", tag="z2_slot", align_bytes=64)
+        hand_on(0, o_bf0)
+        hand_on(1, o_bf1)
+        o_bf3 = finish_on_both(3)
+        hand_on(2, o_bf2)
+        hand_on(3, o_bf3)
         for q in range(4):
             queue = nc.sync if q % 2 == 0 else nc.scalar
             queue.dma_start(out_2[0, 4 * q : 4 * q + 4, :].bitcast(I32), o_scales[32 * q : 32 * q + 4, :].bitcast(I32))

@@ -20,7 +20,7 @@ ADD = mybir.AluOpType.add
 P = 128
 PACK = 4
 LANES = 16
-W1_VECTOR_M = 56
+W1_VECTOR_M = 72
 
 
 def tile_picked_cheb3_none_po_kernel(
@@ -46,14 +46,14 @@ def tile_picked_cheb3_none_po_kernel(
         h_win = [keep.tile([P, S], F32, name="h_win%d" % t, align_bytes=64) for t in range(PACK)]
         ident = keep.tile([P, P], F32, name="ident", align_bytes=64)
 
-        def load_scale_rows(tile, rows):
+        def load_scale_rows(queue, tile, rows):
             for q in range(4):
-                nc.sync.dma_start(tile[32 * q : 32 * q + 4, :].bitcast(I32), rows[0, 4 * q : 4 * q + 4, :].bitcast(I32))
+                queue.dma_start(tile[32 * q : 32 * q + 4, :].bitcast(I32), rows[0, 4 * q : 4 * q + 4, :].bitcast(I32))
 
         nc.gpsimd.memset(xs_sb[:].bitcast(I32), 0)
         nc.sync.dma_start(w1_raw[:], w1.rearrange("(p j) c -> p j c", j=PACK))
         nc.sync.dma_start(offs_sb[:], offs)
-        load_scale_rows(xs_sb, x_scales)
+        load_scale_rows(nc.sync, xs_sb, x_scales)
         nc.sync.dma_start(xw_sb[:].bitcast(I32), x_words[0].rearrange("p n t -> p (n t)").bitcast(I32))
         nc.sync.dma_start(p1_sb[:], p1)
         nc.sync.dma_start(gate[:, 0, :], ga)
@@ -63,18 +63,18 @@ def tile_picked_cheb3_none_po_kernel(
             nc.sync.dma_start(w_words[a][:].bitcast(I32), words[0].bitcast(I32))
         for a, rows in enumerate((w2_scales, w3_scales, w4_scales)):
             nc.gpsimd.memset(w_scales[a][:].bitcast(I32), 0)
-            load_scale_rows(w_scales[a], rows)
+            load_scale_rows(nc.sync, w_scales[a], rows)
         for t in range(PACK):
             nc.gpsimd.memset(y_win[t][:, S:], 0.0)
         make_identity(nc, ident[:])
 
+        xs_pick = keep.tile([P, S], U8, name="xs_pick", align_bytes=64)
+        nc.vector.tensor_copy(xs_pick[:], xs_sb[:].indirect(offs_sb[:]))
         w1_bf = keep.tile([P, PACK * H], BF16, name="w1_bf", align_bytes=64)
         w1_dst = w1_bf[:].rearrange("p (t m j) -> p m t j", t=PACK, j=PACK)
         w1_src = w1_raw[:].rearrange("p j (m t) -> p m t j", t=PACK)
         nc.vector.tensor_copy(w1_dst[:, :W1_VECTOR_M], w1_src[:, :W1_VECTOR_M])
         nc.scalar.copy(w1_dst[:, W1_VECTOR_M:], w1_src[:, W1_VECTOR_M:])
-        xs_pick = keep.tile([P, S], U8, name="xs_pick", align_bytes=64)
-        nc.vector.tensor_copy(xs_pick[:], xs_sb[:].indirect(offs_sb[:]))
         w1_codes = keep.tile([P, H], U32, name="w1_codes", align_bytes=64)
         w1_scales = keep.tile([P, H], U8, name="w1_scales", align_bytes=64)
         nc.vector.quantize_mx(out=w1_codes[:].bitcast(FP8X4), scales=w1_scales[:], in_=w1_bf[:])
@@ -88,12 +88,21 @@ def tile_picked_cheb3_none_po_kernel(
 
         blocks = [slice(c * P, (c + 1) * P) for c in range(S // P)]
         y_banks = [psum.tile([P, PACK, P], F32, name="y_bank%d" % c, tag="acc%d" % c) for c in range(S // P)]
-        for t in range(PACK):
+
+        def project(t, c):
+            nc.tensor.matmul_mx(out=y_banks[c][:, t, :], lhsT=w1_codes[:, blocks[t]].bitcast(FP8X4),
+                                lhsT_scale=w1_scales[:, blocks[t]],
+                                rhs=xw_pick[c // 2][:, blocks[c % 2]].bitcast(FP8X4), rhs_scale=xs_pick[:, blocks[c]],
+                                start=True, stop=True)
+
+        for c, block in enumerate(blocks):
+            project(0, c)
+            nc.scalar.mul(y_win[0][:, block], y_banks[c][:, 0, :], -1.0)
+        for c in range(S // P):
+            for t in range(1, PACK):
+                project(t, c)
+        for t in range(1, PACK):
             for c, block in enumerate(blocks):
-                nc.tensor.matmul_mx(out=y_banks[c][:, t, :], lhsT=w1_codes[:, blocks[t]].bitcast(FP8X4),
-                                    lhsT_scale=w1_scales[:, blocks[t]],
-                                    rhs=xw_pick[c // 2][:, blocks[c % 2]].bitcast(FP8X4), rhs_scale=xs_pick[:, block],
-                                    start=True, stop=True)
                 nc.scalar.mul(y_win[t][:, block], y_banks[c][:, t, :], -1.0)
         y_bf = keep.tile([P, S, PACK], BF16, name="y_bf", align_bytes=64)
 
@@ -103,11 +112,10 @@ def tile_picked_cheb3_none_po_kernel(
             nc.vector.quantize_mx(out=codes[:].bitcast(FP8X4), scales=scales[:], in_=values)
             return codes, scales
 
-        out_banks = [psum.tile([P, N], F32, name="out_bank%d" % c, tag="acc%d" % c) for c in range(S // P)]
 
-        def product(a, codes, scales, c):
+        def product(a, codes, scales, c, start=False, stop=False):
             nc.tensor.matmul_mx(out=out_banks[c][:], lhsT=codes.bitcast(FP8X4), lhsT_scale=scales,
-                                rhs=w_words[a][:].bitcast(FP4X4), rhs_scale=w_scales[a][:], start=(a == 0), stop=(a == 2))
+                                rhs=w_words[a][:].bitcast(FP4X4), rhs_scale=w_scales[a][:], start=start, stop=stop)
 
         def add_turned(bank, terms):
             for i, (slot, term) in enumerate(terms):
@@ -132,71 +140,62 @@ def tile_picked_cheb3_none_po_kernel(
             h_back = psum.tile([P, S // P, P], F32, name="h_back", tag="b%d" % (t % 2))
             for c in range(S // P):
                 nc.tensor.transpose(h_back[:, c, :], h_nodes[:, t, c, :], ident[:])
-            nc.scalar.mul(h_win[t][:], h_back[:].rearrange("p c j -> p (c j)"), 2.0)
-            nc.scalar.copy(y_bf[:, blocks[t], :], y_banks[t][:].rearrange("p t j -> p j t"))
-        y_codes, y_scales = quantize("y", y_bf[:].rearrange("p j t -> p (j t)"), S)
-        for c, block in enumerate(blocks):
-            product(0, y_codes[:, block], y_scales[:, block], c)
+            nc.scalar.mul(h_win[t][:, :S], h_back[:].rearrange("p c j -> p (c j)"), 2.0)
+            if t == 0:
+                for c, block in enumerate(blocks):
+                    nc.scalar.copy(y_bf[:, block, :], y_banks[c][:].rearrange("p t j -> p j t"))
 
         h_bf = keep.tile([P, S * PACK], BF16, name="h_bf", tag="h_bf_slot", align_bytes=64)
         for c in range(S // P):
             h_sorted = ring.tile([P, PACK * P], BF16, name="h_sorted", align_bytes=64)
             nc.scalar.copy(h_sorted[:].rearrange("j (u p e) -> j u p e", u=2, e=2),
                            h_nodes[:, :, c, :].rearrange("j (u e) p -> j u p e", u=2))
-            pairs_back(h_sorted, h_bf[:, c * PACK * P : (c + 1) * PACK * P], "b%d" % (c % 2), nc.scalar.copy)
+            pairs_back(h_sorted, h_bf[:, c * PACK * P : (c + 1) * PACK * P], "acc%d" % c, nc.scalar.copy)
 
         o_scales = keep.tile([P, S], U8, name="o_scales", align_bytes=64)
         out_rows = out_0.rearrange("(p t) j -> p t j", t=PACK)
         out_words = out_1[0].rearrange("p n t -> p (n t)").bitcast(I32)
 
-        def neighbours(a, j0, width, tag):
-            entries = slice(j0 // LANES, (j0 + width) // LANES)
-            picked = keep.tile([P, PACK, width], F32, name="picked%d_%d" % (a, j0), tag=tag, align_bytes=64)
-            for t in range(PACK):
-                nc.vector.tensor_tensor(picked[:, t, :], h_win[t][:].indirect((p1_sb, p2_sb)[a][:, entries]),
-                                        gate[:, a, j0 : j0 + width], MULT)
-            return picked
+        out_banks = [psum.tile([P, N], F32, name="out_bank%d" % c, tag="acc%d" % c) for c in range(S // P)]
+        y_codes, y_scales = quantize("y", y_bf[:].rearrange("p j t -> p (j t)"), S)
 
-        def neighbours_by_row(j0, width):
+        def neighbours(j0, width, tag, on_vector):
+            cols = slice(j0, j0 + width)
             entries = slice(j0 // LANES, (j0 + width) // LANES)
-            both = [keep.tile([P, PACK, width], F32, name="both%d_%d" % (a, j0), align_bytes=64) for a in range(2)]
+            picked = keep.tile([P, 2, PACK, width], F32, name="picked%d" % j0, tag=tag, align_bytes=64)
+            partial = keep.tile([P, PACK, width], F32, name="partial%d" % j0, tag="partial%d" % j0, align_bytes=64)
             for t in range(PACK):
-                for a in range(2):
-                    nc.vector.tensor_tensor(both[a][:, t, :], h_win[t][:].indirect((p1_sb, p2_sb)[a][:, entries]),
-                                            gate[:, a, j0 : j0 + width], MULT)
-            return both
+                by_p1 = picked[:, 0, t, :]
+                nc.vector.tensor_tensor(by_p1, h_win[t][:].indirect(p1_sb[:, entries]), gate[:, 0, cols], MULT)
+                nc.vector.tensor_tensor(picked[:, 1, t, :], h_win[t][:].indirect(p2_sb[:, entries]), gate[:, 1, cols], MULT)
+                if on_vector:
+                    nc.vector.tensor_tensor(partial[:, t, :], by_p1, y_win[t][:, cols], ADD)
+            return picked, partial
 
-        def sum_on_tensor(c, za, zb, local, tag):
-            zt = psum.tile([P, PACK, P], F32, name="zt", tag="a%d" % (c % 2))
+        def sum_on_vector(j0, width, picked, partial):
+            z_bf = keep.tile([P, PACK * width], BF16, name="z_bf%d" % j0, tag="z%d_slot" % j0, align_bytes=64)
+            nc.vector.tensor_tensor(z_bf[:].rearrange("p (c i t) -> p c t i", i=4, t=PACK),
+                                    partial[:].rearrange("p t (c i) -> p c t i", i=4),
+                                    picked[:, 1].rearrange("p t (c i) -> p c t i", i=4), ADD)
+            return z_bf
+
+        def sum_on_tensor(c, picked, local, bank):
+            zt = psum.tile([P, PACK, P], F32, name="zt", tag=bank)
             terms = [(t, y_win[t][:, blocks[c]]) for t in range(PACK)]
             for t in range(PACK):
-                terms = terms + [(t, za[:, t, local]), (t, zb[:, t, local])]
+                terms = terms + [(t, picked[:, 0, t, local]), (t, picked[:, 1, t, local])]
             add_turned(zt, terms)
             z_sorted = ring.tile([P, PACK * P], BF16, name="z_sorted", align_bytes=64)
             nc.scalar.copy(z_sorted[:].rearrange("j (u p e) -> j u p e", u=2, e=2),
                            zt[:].rearrange("j (u e) p -> j u p e", u=2))
-            z_bf = keep.tile([P, PACK * P], BF16, name="z_bf%d" % c, tag=tag, align_bytes=64)
-            pairs_back(z_sorted, z_bf[:], "b0", nc.scalar.copy)
+            z_bf = keep.tile([P, PACK * P], BF16, name="z_bf%d" % c, tag="z%d_slot" % (c * P), align_bytes=64)
+            pairs_back(z_sorted, z_bf[:], bank, nc.scalar.copy)
             return z_bf
 
-        def sum_on_vector(c, za, zb):
-            zs = keep.tile([P, PACK, P], F32, name="zs", tag="z2_slot", align_bytes=64)
-            for t in range(PACK):
-                nc.vector.tensor_tensor(zs[:, t, :], za[:, t, :], y_win[t][:, blocks[c]], ADD)
-            z_bf = ring.tile([P, PACK * P], BF16, name="z_bf", align_bytes=64)
-            nc.vector.tensor_tensor(z_bf[:].rearrange("p (c i t) -> p c t i", i=4, t=PACK),
-                                    zs[:].rearrange("p t (c i) -> p c t i", i=4),
-                                    zb[:].rearrange("p t (c i) -> p c t i", i=4), ADD)
-            return z_bf
-
-        def last_product(c, z_bf):
-            z_codes, z_scales = quantize("z%d" % c, z_bf[:], P)
-            product(2, z_codes[:], z_scales[:], c)
-
-        def turn_back(c):
+        def turn_back(c, copy):
             turned = ring.tile([P, PACK, P], F32, name="turned", align_bytes=64)
-            nc.scalar.copy(turned[:], out_banks[c][:].rearrange("j (p t) -> j t p", t=PACK))
-            back = psum.tile([P, PACK, P], F32, name="back", tag=("b1", "a1")[c % 2])
+            copy(turned[:], out_banks[c][:].rearrange("j (p t) -> j t p", t=PACK))
+            back = psum.tile([P, PACK, P], F32, name="back", tag=("b1", "a1", "b0", "b1")[c])
             for t in range(PACK):
                 nc.tensor.transpose(back[:, t, :], turned[:, t, :], ident[:])
             return turned, back
@@ -207,14 +206,14 @@ def tile_picked_cheb3_none_po_kernel(
             nc.sync.dma_start(out_rows[:, :, blocks[c]], o_f32[:])
 
         def finish_on_scalar(c):
-            turned, back = turn_back(c)
+            turned, back = turn_back(c, nc.scalar.copy)
             o_bf = ring.tile([P, PACK * P], BF16, name="o_bf", align_bytes=64)
             nc.scalar.copy(o_bf[:].rearrange("p (j t) -> p j t", t=PACK), back[:].rearrange("p t j -> p j t"))
             store_rows(c, back)
             return o_bf
 
         def finish_on_both(c):
-            turned, back = turn_back(c)
+            turned, back = turn_back(c, nc.vector.tensor_copy)
             o_sorted = ring.tile([P, PACK * P], BF16, name="o_sorted", align_bytes=64)
             nc.vector.tensor_copy(o_sorted[:].rearrange("j (u p e) -> j u p e", u=2, e=2),
                                   turned[:].rearrange("j (u e) p -> j u p e", u=2))
@@ -227,31 +226,29 @@ def tile_picked_cheb3_none_po_kernel(
             nc.vector.quantize_mx(out=o_codes[:, blocks[c]].bitcast(FP8X4), scales=o_scales[:, blocks[c]], in_=o_bf[:])
             nc.sync.dma_start(out_words[:, blocks[c]], o_codes[:, blocks[c]].bitcast(I32))
 
-        za01, zb01 = neighbours_by_row(0, 2 * P)
-        z_bf0 = sum_on_tensor(0, za01, zb01, blocks[0], "z0_slot")
-        z_bf1 = sum_on_tensor(1, za01, zb01, blocks[1], "z1_slot")
-        za2 = neighbours(0, 2 * P, P, "za2")
-        h_codes, h_scales = quantize("h", h_bf[:], S)
         for c, block in enumerate(blocks):
-            product(1, h_codes[:, block], h_scales[:, block], c)
-        zb2 = neighbours(1, 2 * P, P, "h_bf_slot")
-        last_product(0, z_bf0)
-        last_product(1, z_bf1)
-        z_bf2 = sum_on_tensor(2, za2, zb2, blocks[0], "z2_slot")
-        o_bf0 = finish_on_scalar(0)
-        o_bf1 = finish_on_scalar(1)
-        za3 = neighbours(0, 3 * P, P, "z0_slot")
-        zb3 = neighbours(1, 3 * P, P, "z1_slot")
-        last_product(2, z_bf2)
-        o_bf2 = finish_on_scalar(2)
-        z_bf3 = sum_on_vector(3, za3, zb3)
-        last_product(3, z_bf3)
-        o_codes = keep.tile([P, S], U32, name="o_codes", tag="z2_slot", align_bytes=64)
-        hand_on(0, o_bf0)
-        hand_on(1, o_bf1)
-        o_bf3 = finish_on_both(3)
-        hand_on(2, o_bf2)
-        hand_on(3, o_bf3)
+            product(0, y_codes[:, block], y_scales[:, block], c, start=True)
+        picked, partial = neighbours(0, P, "picked0", False)
+        z_bf0 = sum_on_tensor(0, picked, blocks[0], "a0")
+        picked, partial = neighbours(P, 2 * P, "picked1", True)
+        z_codes, z_scales = quantize("z0", z_bf0[:], P)
+        product(2, z_codes[:], z_scales[:], 0)
+        z_codes, z_scales = quantize("z1", sum_on_vector(P, 2 * P, picked, partial)[:], 2 * P)
+        for c in range(1, 3):
+            product(2, z_codes[:, blocks[c - 1]], z_scales[:, blocks[c - 1]], c)
+        h_codes, h_scales = quantize("h", h_bf[:], S)
+        rounded = []
+        for c in range(3):
+            product(1, h_codes[:, blocks[c]], h_scales[:, blocks[c]], c, stop=True)
+            rounded.append(finish_on_scalar(c))
+        product(1, h_codes[:, blocks[3]], h_scales[:, blocks[3]], 3)
+        picked, partial = neighbours(3 * P, P, "h_bf_slot", True)
+        z_codes, z_scales = quantize("z3", sum_on_vector(3 * P, P, picked, partial)[:], P)
+        product(2, z_codes[:], z_scales[:], 3, stop=True)
+        o_codes = keep.tile([P, S], U32, name="o_codes", tag="partial%d" % (3 * P), align_bytes=64)
+        for c, o_bf in enumerate(rounded):
+            hand_on(c, o_bf)
+        hand_on(3, finish_on_both(3))
         for q in range(4):
             queue = nc.sync if q % 2 == 0 else nc.scalar
             queue.dma_start(out_2[0, 4 * q : 4 * q + 4, :].bitcast(I32), o_scales[32 * q : 32 * q + 4, :].bitcast(I32))

@@ -20,7 +20,7 @@ ADD = mybir.AluOpType.add
 P = 128
 PACK = 4
 LANES = 16
-W1_VECTOR_M = 72
+W1_VECTOR_M = 64
 
 
 def tile_picked_cheb3_none_po_kernel(
@@ -51,9 +51,9 @@ def tile_picked_cheb3_none_po_kernel(
                 queue.dma_start(tile[32 * q : 32 * q + 4, :].bitcast(I32), rows[0, 4 * q : 4 * q + 4, :].bitcast(I32))
 
         nc.gpsimd.memset(xs_sb[:].bitcast(I32), 0)
-        nc.sync.dma_start(w1_raw[:], w1.rearrange("(p j) c -> p j c", j=PACK))
         nc.sync.dma_start(offs_sb[:], offs)
         load_scale_rows(nc.sync, xs_sb, x_scales)
+        nc.sync.dma_start(w1_raw[:], w1.rearrange("(p j) c -> p j c", j=PACK))
         nc.sync.dma_start(xw_sb[:].bitcast(I32), x_words[0].rearrange("p n t -> p (n t)").bitcast(I32))
         nc.sync.dma_start(p1_sb[:], p1)
         nc.sync.dma_start(gate[:, 0, :], ga)
@@ -128,7 +128,9 @@ def tile_picked_cheb3_none_po_kernel(
                 nc.tensor.transpose(pairs[:, u, :], sorted_bf[:].bitcast(F32)[:, blocks[u]], ident[:])
             copy(dst.bitcast(F32).rearrange("p (j u) -> p j u", u=2), pairs[:].rearrange("p u j -> p j u"))
 
-        h_nodes = keep.tile([P, PACK, S // P, P], F32, name="h_nodes", align_bytes=64)
+        for c, block in enumerate(blocks):
+            nc.scalar.copy(y_bf[:, block, :], y_banks[c][:].rearrange("p t j -> p j t"))
+        h_banks = [psum.tile([P, PACK, P], F32, name="h_bank%d" % c, tag="acc%d" % c) for c in range(S // P)]
         for t in range(PACK):
             first = ring.tile([P, S], F32, name="first", align_bytes=64)
             second = ring.tile([P, S], F32, name="second", align_bytes=64)
@@ -136,61 +138,58 @@ def tile_picked_cheb3_none_po_kernel(
             nc.vector.tensor_tensor(second[:], y_win[t][:].indirect(p2_sb[:]), gate[:, 1, :], MULT)
             summed = psum.tile([P, S // P, P], F32, name="summed", tag="a%d" % (t % 2))
             add_turned(summed, [(c, term[:, block]) for term in (first, second) for c, block in enumerate(blocks)])
-            nc.scalar.mul(h_nodes[:, t], summed[:], -1.0)
-            h_back = psum.tile([P, S // P, P], F32, name="h_back", tag="b%d" % (t % 2))
-            for c in range(S // P):
-                nc.tensor.transpose(h_back[:, c, :], h_nodes[:, t, c, :], ident[:])
-            nc.scalar.mul(h_win[t][:, :S], h_back[:].rearrange("p c j -> p (c j)"), 2.0)
-            if t == 0:
-                for c, block in enumerate(blocks):
-                    nc.scalar.copy(y_bf[:, block, :], y_banks[c][:].rearrange("p t j -> p j t"))
-
+            h_nodes = ring.tile([P, S // P, P], F32, name="h_nodes", align_bytes=64)
+            nc.scalar.mul(h_nodes[:], summed[:], -1.0)
+            for c, block in enumerate(blocks):
+                nc.tensor.transpose(h_banks[c][:, t, :], h_nodes[:, c, :], ident[:])
+                nc.scalar.mul(h_win[t][:, block], h_banks[c][:, t, :], 2.0)
         h_bf = keep.tile([P, S * PACK], BF16, name="h_bf", tag="h_bf_slot", align_bytes=64)
-        for c in range(S // P):
-            h_sorted = ring.tile([P, PACK * P], BF16, name="h_sorted", align_bytes=64)
-            nc.scalar.copy(h_sorted[:].rearrange("j (u p e) -> j u p e", u=2, e=2),
-                           h_nodes[:, :, c, :].rearrange("j (u e) p -> j u p e", u=2))
-            pairs_back(h_sorted, h_bf[:, c * PACK * P : (c + 1) * PACK * P], "acc%d" % c, nc.scalar.copy)
+        for c, block in enumerate(blocks):
+            nc.scalar.copy(h_bf[:].rearrange("p (j t) -> p j t", t=PACK)[:, block, :], h_banks[c][:].rearrange("p t j -> p j t"))
 
         o_scales = keep.tile([P, S], U8, name="o_scales", align_bytes=64)
         out_rows = out_0.rearrange("(p t) j -> p t j", t=PACK)
         out_words = out_1[0].rearrange("p n t -> p (n t)").bitcast(I32)
 
-        out_banks = [psum.tile([P, N], F32, name="out_bank%d" % c, tag="acc%d" % c) for c in range(S // P)]
         y_codes, y_scales = quantize("y", y_bf[:].rearrange("p j t -> p (j t)"), S)
 
-        def neighbours(j0, width, tag, on_vector):
-            cols = slice(j0, j0 + width)
+        def gather_pair(dst, t, j0, width):
             entries = slice(j0 // LANES, (j0 + width) // LANES)
-            picked = keep.tile([P, 2, PACK, width], F32, name="picked%d" % j0, tag=tag, align_bytes=64)
-            partial = keep.tile([P, PACK, width], F32, name="partial%d" % j0, tag="partial%d" % j0, align_bytes=64)
-            for t in range(PACK):
-                by_p1 = picked[:, 0, t, :]
-                nc.vector.tensor_tensor(by_p1, h_win[t][:].indirect(p1_sb[:, entries]), gate[:, 0, cols], MULT)
-                nc.vector.tensor_tensor(picked[:, 1, t, :], h_win[t][:].indirect(p2_sb[:, entries]), gate[:, 1, cols], MULT)
-                if on_vector:
-                    nc.vector.tensor_tensor(partial[:, t, :], by_p1, y_win[t][:, cols], ADD)
-            return picked, partial
+            for a, lists in enumerate((p1_sb, p2_sb)):
+                nc.vector.tensor_tensor(dst[a], h_win[t][:].indirect(lists[:, entries]), gate[:, a, j0 : j0 + width], MULT)
 
-        def sum_on_vector(j0, width, picked, partial):
-            z_bf = keep.tile([P, PACK * width], BF16, name="z_bf%d" % j0, tag="z%d_slot" % j0, align_bytes=64)
+        def sum_on_vector(c, tag, late_tag=None, late_from=PACK, between=None):
+            picked = keep.tile([P, 2, PACK, P], F32, name="picked%d" % c, tag=tag, align_bytes=64)
+            partial = keep.tile([P, PACK, P], F32, name="partial%d" % c, tag="partial%d" % c, align_bytes=64)
+            for t in range(PACK):
+                if t == late_from:
+                    between()
+                    late = keep.tile([P, PACK, P], F32, name="late%d" % c, tag=late_tag, align_bytes=64)
+                by_p1 = picked[:, 0, t, :] if t < late_from else late[:, t, :]
+                gather_pair((by_p1, picked[:, 1, t, :]), t, c * P, P)
+                nc.vector.tensor_tensor(partial[:, t, :], by_p1, y_win[t][:, blocks[c]], ADD)
+            z_bf = keep.tile([P, PACK * P], BF16, name="z_bf%d" % c, tag="z%d_slot" % c, align_bytes=64)
             nc.vector.tensor_tensor(z_bf[:].rearrange("p (c i t) -> p c t i", i=4, t=PACK),
                                     partial[:].rearrange("p t (c i) -> p c t i", i=4),
                                     picked[:, 1].rearrange("p t (c i) -> p c t i", i=4), ADD)
             return z_bf
 
-        def sum_on_tensor(c, picked, local, bank):
+        def sum_on_tensor(c, rows, bank, pair_bank):
             zt = psum.tile([P, PACK, P], F32, name="zt", tag=bank)
             terms = [(t, y_win[t][:, blocks[c]]) for t in range(PACK)]
             for t in range(PACK):
-                terms = terms + [(t, picked[:, 0, t, local]), (t, picked[:, 1, t, local])]
+                terms = terms + [(t, rows[t][:, a, blocks[c]]) for a in range(2)]
             add_turned(zt, terms)
             z_sorted = ring.tile([P, PACK * P], BF16, name="z_sorted", align_bytes=64)
             nc.scalar.copy(z_sorted[:].rearrange("j (u p e) -> j u p e", u=2, e=2),
                            zt[:].rearrange("j (u e) p -> j u p e", u=2))
-            z_bf = keep.tile([P, PACK * P], BF16, name="z_bf%d" % c, tag="z%d_slot" % (c * P), align_bytes=64)
-            pairs_back(z_sorted, z_bf[:], bank, nc.scalar.copy)
+            z_bf = keep.tile([P, PACK * P], BF16, name="z_bf%d" % c, tag="z%d_slot" % c, align_bytes=64)
+            pairs_back(z_sorted, z_bf[:], pair_bank, nc.scalar.copy)
             return z_bf
+
+        def last_product(c, z_bf):
+            z_codes, z_scales = quantize("z%d" % c, z_bf[:], P)
+            product(2, z_codes[:], z_scales[:], c, stop=True)
 
         def turn_back(c, copy):
             turned = ring.tile([P, PACK, P], F32, name="turned", align_bytes=64)
@@ -226,27 +225,27 @@ def tile_picked_cheb3_none_po_kernel(
             nc.vector.quantize_mx(out=o_codes[:, blocks[c]].bitcast(FP8X4), scales=o_scales[:, blocks[c]], in_=o_bf[:])
             nc.sync.dma_start(out_words[:, blocks[c]], o_codes[:, blocks[c]].bitcast(I32))
 
+        rows = []
+        for t in range(PACK):
+            row = keep.tile([P, 2, 2 * P], F32, name="row%d" % t, align_bytes=64)
+            gather_pair((row[:, 0, :], row[:, 1, :]), t, 0, 2 * P)
+            rows.append(row)
+        sums = [sum_on_tensor(c, rows, ("a0", "a1")[c], "acc%d" % (c + 0)) for c in range(2)]
+        out_banks = [psum.tile([P, N], F32, name="out_bank%d" % c, tag="acc%d" % c) for c in range(S // P)]
         for c, block in enumerate(blocks):
             product(0, y_codes[:, block], y_scales[:, block], c, start=True)
-        picked, partial = neighbours(0, P, "picked0", False)
-        z_bf0 = sum_on_tensor(0, picked, blocks[0], "a0")
-        picked, partial = neighbours(P, 2 * P, "picked1", True)
-        z_codes, z_scales = quantize("z0", z_bf0[:], P)
-        product(2, z_codes[:], z_scales[:], 0)
-        z_codes, z_scales = quantize("z1", sum_on_vector(P, 2 * P, picked, partial)[:], 2 * P)
-        for c in range(1, 3):
-            product(2, z_codes[:, blocks[c - 1]], z_scales[:, blocks[c - 1]], c)
-        h_codes, h_scales = quantize("h", h_bf[:], S)
+        hq = []
+        sums.append(sum_on_vector(2, "picked2", "h_bf_slot", 1, lambda: hq.extend(quantize("h", h_bf[:], S))))
+        h_codes, h_scales = hq
         rounded = []
         for c in range(3):
-            product(1, h_codes[:, blocks[c]], h_scales[:, blocks[c]], c, stop=True)
-            rounded.append(finish_on_scalar(c))
+            product(1, h_codes[:, blocks[c]], h_scales[:, blocks[c]], c)
+            last_product(c, sums[c])
+            rounded.append((c, finish_on_scalar(c)))
         product(1, h_codes[:, blocks[3]], h_scales[:, blocks[3]], 3)
-        picked, partial = neighbours(3 * P, P, "h_bf_slot", True)
-        z_codes, z_scales = quantize("z3", sum_on_vector(3 * P, P, picked, partial)[:], P)
-        product(2, z_codes[:], z_scales[:], 3, stop=True)
-        o_codes = keep.tile([P, S], U32, name="o_codes", tag="partial%d" % (3 * P), align_bytes=64)
-        for c, o_bf in enumerate(rounded):
+        last_product(3, sum_on_vector(3, "h_bf_slot"))
+        o_codes = keep.tile([P, S], U32, name="o_codes", tag="partial3", align_bytes=64)
+        for c, o_bf in rounded:
             hand_on(c, o_bf)
         hand_on(3, finish_on_both(3))
         for q in range(4):

@@ -4,7 +4,7 @@ import concourse.mybir as mybir
 from concourse.masks import make_identity
 
 K, T, S, H, N = 512, 2048, 512, 512, 512
-FLOPS = 4 * 2 * 512 * 512 * 512
+FLOPS = 2 * K * H * S + 3 * 2 * H * N * S
 
 F32 = mybir.dt.float32
 BF16 = mybir.dt.bfloat16
@@ -20,7 +20,13 @@ ADD = mybir.AluOpType.add
 P = 128
 PACK = 4
 LANES = 16
-W1_VECTOR_M = 64
+QUADRANTS = 4
+BLOCKS = S // P
+LAST = BLOCKS - 1
+ON_TENSOR = 2
+RUN = 4
+W1_ON_VECTOR = 64
+RING = 4
 
 
 def tile_picked_cheb3_none_po_kernel(
@@ -28,9 +34,10 @@ def tile_picked_cheb3_none_po_kernel(
     offs, p1, p2, out_0, out_1, out_2,
 ):
     nc = tc.nc
+    blocks = [slice(c * P, (c + 1) * P) for c in range(BLOCKS)]
     with ExitStack() as ctx:
         keep = ctx.enter_context(tc.tile_pool(name="keep", bufs=1))
-        ring = ctx.enter_context(tc.tile_pool(name="ring", bufs=4))
+        ring = ctx.enter_context(tc.tile_pool(name="ring", bufs=RING))
         psum = ctx.enter_context(tc.psum_pool(name="psum", bufs=1))
 
         offs_sb = keep.tile([P, S // LANES], U16, name="offs_sb")
@@ -42,17 +49,17 @@ def tile_picked_cheb3_none_po_kernel(
         gate = keep.tile([P, 2, S], F32, name="gate", align_bytes=64)
         w_words = [keep.tile([P, 2 * N], U8, name="w_words%d" % a, align_bytes=64) for a in range(3)]
         w_scales = [keep.tile([P, N], U8, name="w_scales%d" % a, align_bytes=64) for a in range(3)]
-        y_win = [keep.tile([P, 2 * S], F32, name="y_win%d" % t, align_bytes=64) for t in range(PACK)]
-        h_win = [keep.tile([P, S], F32, name="h_win%d" % t, align_bytes=64) for t in range(PACK)]
+        neg_y = [keep.tile([P, 2 * S], F32, name="neg_y%d" % t, align_bytes=64) for t in range(PACK)]
+        two_h = [keep.tile([P, S], F32, name="two_h%d" % t, align_bytes=64) for t in range(PACK)]
         ident = keep.tile([P, P], F32, name="ident", align_bytes=64)
 
-        def load_scale_rows(queue, tile, rows):
-            for q in range(4):
-                queue.dma_start(tile[32 * q : 32 * q + 4, :].bitcast(I32), rows[0, 4 * q : 4 * q + 4, :].bitcast(I32))
+        def load_scale_rows(tile, rows):
+            for q in range(QUADRANTS):
+                nc.sync.dma_start(tile[32 * q : 32 * q + 4, :].bitcast(I32), rows[0, 4 * q : 4 * q + 4, :].bitcast(I32))
 
         nc.gpsimd.memset(xs_sb[:].bitcast(I32), 0)
         nc.sync.dma_start(offs_sb[:], offs)
-        load_scale_rows(nc.sync, xs_sb, x_scales)
+        load_scale_rows(xs_sb, x_scales)
         nc.sync.dma_start(w1_raw[:], w1.rearrange("(p j) c -> p j c", j=PACK))
         nc.sync.dma_start(xw_sb[:].bitcast(I32), x_words[0].rearrange("p n t -> p (n t)").bitcast(I32))
         nc.sync.dma_start(p1_sb[:], p1)
@@ -61,33 +68,35 @@ def tile_picked_cheb3_none_po_kernel(
         nc.sync.dma_start(gate[:, 1, :], gb)
         for a, words in enumerate((w2_words, w3_words, w4_words)):
             nc.sync.dma_start(w_words[a][:].bitcast(I32), words[0].bitcast(I32))
-        for a, rows in enumerate((w2_scales, w3_scales, w4_scales)):
+        for a, scale_rows in enumerate((w2_scales, w3_scales, w4_scales)):
             nc.gpsimd.memset(w_scales[a][:].bitcast(I32), 0)
-            load_scale_rows(nc.sync, w_scales[a], rows)
+            load_scale_rows(w_scales[a], scale_rows)
         for t in range(PACK):
-            nc.gpsimd.memset(y_win[t][:, S:], 0.0)
+            nc.vector.memset(neg_y[t][:, S:], 0.0)
         make_identity(nc, ident[:])
+
+        def quantize(name, values, width):
+            codes = keep.tile([P, width], U32, name=name + "_codes", align_bytes=64)
+            scales = keep.tile([P, width], U8, name=name + "_scales", align_bytes=64)
+            nc.vector.quantize_mx(out=codes[:].bitcast(FP8X4), scales=scales[:], in_=values)
+            return codes, scales
 
         xs_pick = keep.tile([P, S], U8, name="xs_pick", align_bytes=64)
         nc.vector.tensor_copy(xs_pick[:], xs_sb[:].indirect(offs_sb[:]))
         w1_bf = keep.tile([P, PACK * H], BF16, name="w1_bf", align_bytes=64)
         w1_dst = w1_bf[:].rearrange("p (t m j) -> p m t j", t=PACK, j=PACK)
         w1_src = w1_raw[:].rearrange("p j (m t) -> p m t j", t=PACK)
-        nc.vector.tensor_copy(w1_dst[:, :W1_VECTOR_M], w1_src[:, :W1_VECTOR_M])
-        nc.scalar.copy(w1_dst[:, W1_VECTOR_M:], w1_src[:, W1_VECTOR_M:])
-        w1_codes = keep.tile([P, H], U32, name="w1_codes", align_bytes=64)
-        w1_scales = keep.tile([P, H], U8, name="w1_scales", align_bytes=64)
-        nc.vector.quantize_mx(out=w1_codes[:].bitcast(FP8X4), scales=w1_scales[:], in_=w1_bf[:])
-        half = S // 2
+        nc.vector.tensor_copy(w1_dst[:, :W1_ON_VECTOR], w1_src[:, :W1_ON_VECTOR])
+        nc.scalar.copy(w1_dst[:, W1_ON_VECTOR:], w1_src[:, W1_ON_VECTOR:])
+        w1_codes, w1_scales = quantize("w1", w1_bf[:], H)
         xw_pick = []
         for u in range(2):
-            picked = keep.tile([P, half], U32, name="xw_pick%d" % u, align_bytes=64)
-            entries = slice(u * half // LANES, (u + 1) * half // LANES)
-            nc.vector.tensor_copy(picked[:], xw_sb[:].indirect(offs_sb[:, entries]))
-            xw_pick.append(picked)
+            words_half = keep.tile([P, 2 * P], U32, name="xw_pick%d" % u, align_bytes=64)
+            entries = slice(u * 2 * P // LANES, (u + 1) * 2 * P // LANES)
+            nc.vector.tensor_copy(words_half[:], xw_sb[:].indirect(offs_sb[:, entries]))
+            xw_pick.append(words_half)
 
-        blocks = [slice(c * P, (c + 1) * P) for c in range(S // P)]
-        y_banks = [psum.tile([P, PACK, P], F32, name="y_bank%d" % c, tag="acc%d" % c) for c in range(S // P)]
+        y_banks = [psum.tile([P, PACK, P], F32, name="y_bank%d" % c, tag="block%d" % c) for c in range(BLOCKS)]
 
         def project(t, c):
             nc.tensor.matmul_mx(out=y_banks[c][:, t, :], lhsT=w1_codes[:, blocks[t]].bitcast(FP8X4),
@@ -97,157 +106,167 @@ def tile_picked_cheb3_none_po_kernel(
 
         for c, block in enumerate(blocks):
             project(0, c)
-            nc.scalar.mul(y_win[0][:, block], y_banks[c][:, 0, :], -1.0)
-        for c in range(S // P):
+            if c == LAST:
+                nc.vector.tensor_scalar_mul(neg_y[0][:, block], y_banks[c][:, 0, :], -1.0)
+            else:
+                nc.scalar.mul(neg_y[0][:, block], y_banks[c][:, 0, :], -1.0)
+        for c in range(BLOCKS):
             for t in range(1, PACK):
                 project(t, c)
         for t in range(1, PACK):
             for c, block in enumerate(blocks):
-                nc.scalar.mul(y_win[t][:, block], y_banks[c][:, t, :], -1.0)
+                nc.scalar.mul(neg_y[t][:, block], y_banks[c][:, t, :], -1.0)
         y_bf = keep.tile([P, S, PACK], BF16, name="y_bf", align_bytes=64)
-
-        def quantize(name, values, width):
-            codes = keep.tile([P, width], U32, name=name + "_codes", align_bytes=64)
-            scales = keep.tile([P, width], U8, name=name + "_scales", align_bytes=64)
-            nc.vector.quantize_mx(out=codes[:].bitcast(FP8X4), scales=scales[:], in_=values)
-            return codes, scales
-
-
-        def product(a, codes, scales, c, start=False, stop=False):
-            nc.tensor.matmul_mx(out=out_banks[c][:], lhsT=codes.bitcast(FP8X4), lhsT_scale=scales,
-                                rhs=w_words[a][:].bitcast(FP4X4), rhs_scale=w_scales[a][:], start=start, stop=stop)
-
-        def add_turned(bank, terms):
-            for i, (slot, term) in enumerate(terms):
-                nc.tensor.matmul(bank[:, slot, :], lhsT=term, rhs=ident[:], is_transpose=True,
-                                 start=(i == 0), stop=(i == len(terms) - 1))
-
-        def pairs_back(sorted_bf, dst, tag, copy):
-            pairs = psum.tile([P, 2, P], F32, name="pairs", tag=tag)
-            for u in range(2):
-                nc.tensor.transpose(pairs[:, u, :], sorted_bf[:].bitcast(F32)[:, blocks[u]], ident[:])
-            copy(dst.bitcast(F32).rearrange("p (j u) -> p j u", u=2), pairs[:].rearrange("p u j -> p j u"))
-
         for c, block in enumerate(blocks):
             nc.scalar.copy(y_bf[:, block, :], y_banks[c][:].rearrange("p t j -> p j t"))
-        h_banks = [psum.tile([P, PACK, P], F32, name="h_bank%d" % c, tag="acc%d" % c) for c in range(S // P)]
+
+        def add_turned(bank, terms):
+            for i, (quarter, term) in enumerate(terms):
+                nc.tensor.matmul(bank[:, quarter, :], lhsT=term, rhs=ident[:], is_transpose=True,
+                                 start=(i == 0), stop=(i == len(terms) - 1))
+
+        def sort_pairs(copy, name, by_node):
+            in_pairs = ring.tile([P, PACK * P], BF16, name=name, align_bytes=64)
+            copy(in_pairs[:].rearrange("j (u p e) -> j u p e", u=2, e=2), by_node.rearrange("j (u e) p -> j u p e", u=2))
+            return in_pairs
+
+        def turn_pairs(copy, in_pairs, dst, tag):
+            pairs = psum.tile([P, 2, P], F32, name="pairs", tag=tag)
+            for u in range(2):
+                nc.tensor.transpose(pairs[:, u, :], in_pairs[:].bitcast(F32)[:, blocks[u]], ident[:])
+            copy(dst.bitcast(F32).rearrange("p (j u) -> p j u", u=2), pairs[:].rearrange("p u j -> p j u"))
+
+        h_banks = [psum.tile([P, PACK, P], F32, name="h_bank%d" % c, tag="block%d" % c) for c in range(BLOCKS)]
         for t in range(PACK):
-            first = ring.tile([P, S], F32, name="first", align_bytes=64)
-            second = ring.tile([P, S], F32, name="second", align_bytes=64)
-            nc.vector.tensor_tensor(first[:], y_win[t][:].indirect(p1_sb[:]), gate[:, 0, :], MULT)
-            nc.vector.tensor_tensor(second[:], y_win[t][:].indirect(p2_sb[:]), gate[:, 1, :], MULT)
-            summed = psum.tile([P, S // P, P], F32, name="summed", tag="a%d" % (t % 2))
-            add_turned(summed, [(c, term[:, block]) for term in (first, second) for c, block in enumerate(blocks)])
-            h_nodes = ring.tile([P, S // P, P], F32, name="h_nodes", align_bytes=64)
-            nc.scalar.mul(h_nodes[:], summed[:], -1.0)
+            y_by_p1 = ring.tile([P, S], F32, name="y_by_p1", align_bytes=64)
+            y_by_p2 = ring.tile([P, S], F32, name="y_by_p2", align_bytes=64)
+            nc.vector.tensor_tensor(y_by_p1[:], neg_y[t][:].indirect(p1_sb[:]), gate[:, 0, :], MULT)
+            nc.vector.tensor_tensor(y_by_p2[:], neg_y[t][:].indirect(p2_sb[:]), gate[:, 1, :], MULT)
+            neg_h_nodes = psum.tile([P, BLOCKS, P], F32, name="neg_h_nodes", tag="sum%d" % (t % 2))
+            add_turned(neg_h_nodes, [(c, term[:, block]) for term in (y_by_p1, y_by_p2) for c, block in enumerate(blocks)])
+            h_nodes = ring.tile([P, BLOCKS, P], F32, name="h_nodes", align_bytes=64)
+            nc.scalar.mul(h_nodes[:], neg_h_nodes[:], -1.0)
             for c, block in enumerate(blocks):
                 nc.tensor.transpose(h_banks[c][:, t, :], h_nodes[:, c, :], ident[:])
-                nc.scalar.mul(h_win[t][:, block], h_banks[c][:, t, :], 2.0)
-        h_bf = keep.tile([P, S * PACK], BF16, name="h_bf", tag="h_bf_slot", align_bytes=64)
+                nc.scalar.mul(two_h[t][:, block], h_banks[c][:, t, :], 2.0)
+        h_bf = keep.tile([P, S, PACK], BF16, name="h_bf", tag="after_h", align_bytes=64)
         for c, block in enumerate(blocks):
-            nc.scalar.copy(h_bf[:].rearrange("p (j t) -> p j t", t=PACK)[:, block, :], h_banks[c][:].rearrange("p t j -> p j t"))
-
-        o_scales = keep.tile([P, S], U8, name="o_scales", align_bytes=64)
-        out_rows = out_0.rearrange("(p t) j -> p t j", t=PACK)
-        out_words = out_1[0].rearrange("p n t -> p (n t)").bitcast(I32)
+            nc.scalar.copy(h_bf[:, block, :], h_banks[c][:].rearrange("p t j -> p j t"))
 
         y_codes, y_scales = quantize("y", y_bf[:].rearrange("p j t -> p (j t)"), S)
 
-        def gather_pair(dst, t, j0, width):
+        def look_up_h(by_p1, by_p2, t, j0, width):
             entries = slice(j0 // LANES, (j0 + width) // LANES)
-            for a, lists in enumerate((p1_sb, p2_sb)):
-                nc.vector.tensor_tensor(dst[a], h_win[t][:].indirect(lists[:, entries]), gate[:, a, j0 : j0 + width], MULT)
+            for a, (dst, lists) in enumerate(((by_p1, p1_sb), (by_p2, p2_sb))):
+                nc.vector.tensor_tensor(dst, two_h[t][:].indirect(lists[:, entries]), gate[:, a, j0 : j0 + width], MULT)
 
-        def sum_on_vector(c, tag, late_tag=None, late_from=PACK, between=None):
-            picked = keep.tile([P, 2, PACK, P], F32, name="picked%d" % c, tag=tag, align_bytes=64)
-            partial = keep.tile([P, PACK, P], F32, name="partial%d" % c, tag="partial%d" % c, align_bytes=64)
-            for t in range(PACK):
-                if t == late_from:
-                    between()
-                    late = keep.tile([P, PACK, P], F32, name="late%d" % c, tag=late_tag, align_bytes=64)
-                by_p1 = picked[:, 0, t, :] if t < late_from else late[:, t, :]
-                gather_pair((by_p1, picked[:, 1, t, :]), t, c * P, P)
-                nc.vector.tensor_tensor(partial[:, t, :], by_p1, y_win[t][:, blocks[c]], ADD)
-            z_bf = keep.tile([P, PACK * P], BF16, name="z_bf%d" % c, tag="z%d_slot" % c, align_bytes=64)
-            nc.vector.tensor_tensor(z_bf[:].rearrange("p (c i t) -> p c t i", i=4, t=PACK),
-                                    partial[:].rearrange("p t (c i) -> p c t i", i=4),
-                                    picked[:, 1].rearrange("p t (c i) -> p c t i", i=4), ADD)
+        def z_on_tensor(c, looked_up):
+            z_nodes = psum.tile([P, PACK, P], F32, name="z_nodes", tag="sum%d" % c)
+            terms = [(t, neg_y[t][:, blocks[c]]) for t in range(PACK)]
+            terms.extend((t, looked_up[t][:, a, blocks[c]]) for t in range(PACK) for a in range(2))
+            add_turned(z_nodes, terms)
+            in_pairs = sort_pairs(nc.scalar.copy, "z_pairs", z_nodes[:])
+            z_bf = keep.tile([P, PACK * P], BF16, name="z_bf%d" % c, align_bytes=64)
+            turn_pairs(nc.scalar.copy, in_pairs, z_bf[:], "block%d" % c)
             return z_bf
 
-        def sum_on_tensor(c, rows, bank, pair_bank):
-            zt = psum.tile([P, PACK, P], F32, name="zt", tag=bank)
-            terms = [(t, y_win[t][:, blocks[c]]) for t in range(PACK)]
-            for t in range(PACK):
-                terms = terms + [(t, rows[t][:, a, blocks[c]]) for a in range(2)]
-            add_turned(zt, terms)
-            z_sorted = ring.tile([P, PACK * P], BF16, name="z_sorted", align_bytes=64)
-            nc.scalar.copy(z_sorted[:].rearrange("j (u p e) -> j u p e", u=2, e=2),
-                           zt[:].rearrange("j (u e) p -> j u p e", u=2))
-            z_bf = keep.tile([P, PACK * P], BF16, name="z_bf%d" % c, tag="z%d_slot" % c, align_bytes=64)
-            pairs_back(z_sorted, z_bf[:], pair_bank, nc.scalar.copy)
+        def z_row_on_vector(c, t, by_p1, by_p2, partial):
+            look_up_h(by_p1, by_p2[:, t, :], t, c * P, P)
+            nc.vector.tensor_tensor(partial[:, t, :], by_p1, neg_y[t][:, blocks[c]], ADD)
+
+        def z_sum_on_vector(c, by_p2, partial):
+            z_bf = keep.tile([P, PACK * P], BF16, name="z_bf%d" % c, align_bytes=64)
+            nc.vector.tensor_tensor(z_bf[:].rearrange("p (g i t) -> p g t i", i=RUN, t=PACK),
+                                    partial[:].rearrange("p t (g i) -> p g t i", i=RUN),
+                                    by_p2.rearrange("p t (g i) -> p g t i", i=RUN), ADD)
             return z_bf
 
-        def last_product(c, z_bf):
+        def product(a, codes, scales, bank, start=False, stop=False):
+            nc.tensor.matmul_mx(out=bank[:], lhsT=codes.bitcast(FP8X4), lhsT_scale=scales,
+                                rhs=w_words[a][:].bitcast(FP4X4), rhs_scale=w_scales[a][:], start=start, stop=stop)
+
+        def close_group(c, z_bf, bank):
             z_codes, z_scales = quantize("z%d" % c, z_bf[:], P)
-            product(2, z_codes[:], z_scales[:], c, stop=True)
+            product(2, z_codes[:], z_scales[:], bank, stop=True)
 
-        def turn_back(c, copy):
-            turned = ring.tile([P, PACK, P], F32, name="turned", align_bytes=64)
-            copy(turned[:], out_banks[c][:].rearrange("j (p t) -> j t p", t=PACK))
-            back = psum.tile([P, PACK, P], F32, name="back", tag=("b1", "a1", "b0", "b1")[c])
+        out_rows = out_0.rearrange("(p t) j -> p t j", t=PACK)
+        out_words = out_1[0].rearrange("p n t -> p (n t)").bitcast(I32)
+
+        def turn_out(c, bank, tag):
+            o_nodes = ring.tile([P, PACK, P], F32, name="o_nodes", align_bytes=64)
+            nc.scalar.copy(o_nodes[:], bank[:].rearrange("j (p t) -> j t p", t=PACK))
+            back = psum.tile([P, PACK, P], F32, name="back", tag=tag)
             for t in range(PACK):
-                nc.tensor.transpose(back[:, t, :], turned[:, t, :], ident[:])
-            return turned, back
-
-        def store_rows(c, back):
+                nc.tensor.transpose(back[:, t, :], o_nodes[:, t, :], ident[:])
+            o_bf = ring.tile([P, PACK * P], BF16, name="o_bf", align_bytes=64)
+            nc.scalar.copy(o_bf[:].rearrange("p (j t) -> p j t", t=PACK), back[:].rearrange("p t j -> p j t"))
             o_f32 = ring.tile([P, PACK, P], F32, name="o_f32", align_bytes=64)
             nc.scalar.copy(o_f32[:], back[:])
             nc.sync.dma_start(out_rows[:, :, blocks[c]], o_f32[:])
-
-        def finish_on_scalar(c):
-            turned, back = turn_back(c, nc.scalar.copy)
-            o_bf = ring.tile([P, PACK * P], BF16, name="o_bf", align_bytes=64)
-            nc.scalar.copy(o_bf[:].rearrange("p (j t) -> p j t", t=PACK), back[:].rearrange("p t j -> p j t"))
-            store_rows(c, back)
             return o_bf
 
-        def finish_on_both(c):
-            turned, back = turn_back(c, nc.vector.tensor_copy)
-            o_sorted = ring.tile([P, PACK * P], BF16, name="o_sorted", align_bytes=64)
-            nc.vector.tensor_copy(o_sorted[:].rearrange("j (u p e) -> j u p e", u=2, e=2),
-                                  turned[:].rearrange("j (u e) p -> j u p e", u=2))
+        def turn_out_last(bank):
+            o_nodes = ring.tile([P, PACK, P], F32, name="o_nodes", align_bytes=64)
+            nc.vector.tensor_copy(o_nodes[:], bank[:].rearrange("j (p t) -> j t p", t=PACK))
+            in_pairs = sort_pairs(nc.vector.tensor_copy, "o_pairs", o_nodes[:])
             o_bf = ring.tile([P, PACK * P], BF16, name="o_bf", align_bytes=64)
-            pairs_back(o_sorted, o_bf[:], "a0", nc.vector.tensor_copy)
-            store_rows(c, back)
+            for u, tag in enumerate(("turn1", "sum1")):
+                half_back = psum.tile([P, 2, P], F32, name="half_back", tag=tag)
+                for e in range(2):
+                    nc.tensor.transpose(half_back[:, e, :], o_nodes[:, 2 * u + e, :], ident[:])
+                o_half = ring.tile([P, 2, P], F32, name="o_half", align_bytes=64)
+                nc.scalar.copy(o_half[:], half_back[:])
+                nc.sync.dma_start(out_rows[:, 2 * u : 2 * u + 2, blocks[LAST]], o_half[:])
+                if u == 0:
+                    turn_pairs(nc.vector.tensor_copy, in_pairs, o_bf[:], "sum0")
             return o_bf
+
+        looked_up = []
+        for t in range(PACK):
+            both = keep.tile([P, 2, ON_TENSOR * P], F32, name="looked_up%d" % t, align_bytes=64)
+            look_up_h(both[:, 0, :], both[:, 1, :], t, 0, ON_TENSOR * P)
+            looked_up.append(both)
+        z_rounded = [z_on_tensor(c, looked_up) for c in range(ON_TENSOR)]
+        out_banks = [psum.tile([P, N], F32, name="out_bank%d" % c, tag="block%d" % c) for c in range(LAST)]
+        for c in range(LAST):
+            product(0, y_codes[:, blocks[c]], y_scales[:, blocks[c]], out_banks[c], start=True)
+
+        mid = ON_TENSOR
+        mid_p1_row0 = keep.tile([P, P], F32, name="mid_p1_row0", align_bytes=64)
+        mid_by_p2 = keep.tile([P, PACK, P], F32, name="mid_by_p2", align_bytes=64)
+        mid_partial = keep.tile([P, PACK, P], F32, name="mid_partial", align_bytes=64)
+        z_row_on_vector(mid, 0, mid_p1_row0[:], mid_by_p2, mid_partial)
+        h_codes, h_scales = quantize("h", h_bf[:].rearrange("p j t -> p (j t)"), S)
+        mid_p1_rest = keep.tile([P, PACK - 1, P], F32, name="mid_p1_rest", tag="after_h", align_bytes=64)
+        for t in range(1, PACK):
+            z_row_on_vector(mid, t, mid_p1_rest[:, t - 1, :], mid_by_p2, mid_partial)
+        z_rounded.append(z_sum_on_vector(mid, mid_by_p2[:], mid_partial))
+
+        o_rounded = []
+        for c, tag in enumerate(("turn1", "sum1", "turn0")):
+            product(1, h_codes[:, blocks[c]], h_scales[:, blocks[c]], out_banks[c])
+            close_group(c, z_rounded[c], out_banks[c])
+            o_rounded.append(turn_out(c, out_banks[c], tag))
+
+        last_bank = psum.tile([P, N], F32, name="last_bank", tag="block%d" % mid)
+        product(0, y_codes[:, blocks[LAST]], y_scales[:, blocks[LAST]], last_bank, start=True)
+        product(1, h_codes[:, blocks[LAST]], h_scales[:, blocks[LAST]], last_bank)
+        last_both = keep.tile([P, 2, PACK, P], F32, name="last_both", tag="after_h", align_bytes=64)
+        last_partial = keep.tile([P, PACK, P], F32, name="last_partial", tag="after_z", align_bytes=64)
+        for t in range(PACK):
+            z_row_on_vector(LAST, t, last_both[:, 0, t, :], last_both[:, 1], last_partial)
+        close_group(LAST, z_sum_on_vector(LAST, last_both[:, 1], last_partial), last_bank)
+
+        o_codes = keep.tile([P, S], U32, name="o_codes", tag="after_z", align_bytes=64)
+        o_scales = keep.tile([P, S], U8, name="o_scales", align_bytes=64)
 
         def hand_on(c, o_bf):
             nc.vector.quantize_mx(out=o_codes[:, blocks[c]].bitcast(FP8X4), scales=o_scales[:, blocks[c]], in_=o_bf[:])
             nc.sync.dma_start(out_words[:, blocks[c]], o_codes[:, blocks[c]].bitcast(I32))
 
-        rows = []
-        for t in range(PACK):
-            row = keep.tile([P, 2, 2 * P], F32, name="row%d" % t, align_bytes=64)
-            gather_pair((row[:, 0, :], row[:, 1, :]), t, 0, 2 * P)
-            rows.append(row)
-        sums = [sum_on_tensor(c, rows, ("a0", "a1")[c], "acc%d" % (c + 0)) for c in range(2)]
-        out_banks = [psum.tile([P, N], F32, name="out_bank%d" % c, tag="acc%d" % c) for c in range(S // P)]
-        for c, block in enumerate(blocks):
-            product(0, y_codes[:, block], y_scales[:, block], c, start=True)
-        hq = []
-        sums.append(sum_on_vector(2, "picked2", "h_bf_slot", 1, lambda: hq.extend(quantize("h", h_bf[:], S))))
-        h_codes, h_scales = hq
-        rounded = []
-        for c in range(3):
-            product(1, h_codes[:, blocks[c]], h_scales[:, blocks[c]], c)
-            last_product(c, sums[c])
-            rounded.append((c, finish_on_scalar(c)))
-        product(1, h_codes[:, blocks[3]], h_scales[:, blocks[3]], 3)
-        last_product(3, sum_on_vector(3, "h_bf_slot"))
-        o_codes = keep.tile([P, S], U32, name="o_codes", tag="partial3", align_bytes=64)
-        for c, o_bf in rounded:
+        for c, o_bf in enumerate(o_rounded):
             hand_on(c, o_bf)
-        hand_on(3, finish_on_both(3))
-        for q in range(4):
+        hand_on(LAST, turn_out_last(last_bank))
+        for q in range(QUADRANTS):
             queue = nc.sync if q % 2 == 0 else nc.scalar
             queue.dma_start(out_2[0, 4 * q : 4 * q + 4, :].bitcast(I32), o_scales[32 * q : 32 * q + 4, :].bitcast(I32))

from contextlib import ExitStack

import concourse.mybir as mybir
from concourse.masks import make_identity

K, T, S, H, N = 512, 2048, 512, 512, 512
FLOPS = 2 * K * H * S + 3 * 2 * H * N * S

F32 = mybir.dt.float32
BF16 = mybir.dt.bfloat16
I32 = mybir.dt.int32
U32 = mybir.dt.uint32
U16 = mybir.dt.uint16
U8 = mybir.dt.uint8
FP8X4 = mybir.dt.float8_e4m3fn_x4
FP4X4 = mybir.dt.float4_e2m1fn_x4
MULT = mybir.AluOpType.mult
ADD = mybir.AluOpType.add

P = 128
PACK = 4
LANES = 16
QUADRANTS = 4
BLOCKS = S // P
LAST = BLOCKS - 1
ON_TENSOR = 2
RUN = 4
W1_ON_VECTOR = 64
RING = 4


def tile_picked_cheb3_none_po_kernel(
    tc, x_words, x_scales, w1, ga, gb, w2_words, w2_scales, w3_words, w3_scales, w4_words, w4_scales,
    offs, p1, p2, out_0, out_1, out_2,
):
    nc = tc.nc
    blocks = [slice(c * P, (c + 1) * P) for c in range(BLOCKS)]
    with ExitStack() as ctx:
        keep = ctx.enter_context(tc.tile_pool(name="keep", bufs=1))
        ring = ctx.enter_context(tc.tile_pool(name="ring", bufs=RING))
        psum = ctx.enter_context(tc.psum_pool(name="psum", bufs=1))

        offs_sb = keep.tile([P, S // LANES], U16, name="offs_sb")
        p1_sb = keep.tile([P, S // LANES], U16, name="p1_sb")
        p2_sb = keep.tile([P, S // LANES], U16, name="p2_sb")
        xs_sb = keep.tile([P, T], U8, name="xs_sb", align_bytes=64)
        xw_sb = keep.tile([P, T], U32, name="xw_sb", align_bytes=64)
        w1_raw = keep.tile([P, PACK, H], F32, name="w1_raw", align_bytes=64)
        gate = keep.tile([P, 2, S], F32, name="gate", align_bytes=64)
        w_words = [keep.tile([P, 2 * N], U8, name="w_words%d" % a, align_bytes=64) for a in range(3)]
        w_scales = [keep.tile([P, N], U8, name="w_scales%d" % a, align_bytes=64) for a in range(3)]
        neg_y = [keep.tile([P, 2 * S], F32, name="neg_y%d" % t, align_bytes=64) for t in range(PACK)]
        two_h = [keep.tile([P, S], F32, name="two_h%d" % t, align_bytes=64) for t in range(PACK)]
        ident = keep.tile([P, P], F32, name="ident", align_bytes=64)

        def load_scale_rows(tile, rows):
            for q in range(QUADRANTS):
                nc.sync.dma_start(tile[32 * q : 32 * q + 4, :].bitcast(I32), rows[0, 4 * q : 4 * q + 4, :].bitcast(I32))

        nc.gpsimd.memset(xs_sb[:].bitcast(I32), 0)
        nc.sync.dma_start(offs_sb[:], offs)
        load_scale_rows(xs_sb, x_scales)
        nc.sync.dma_start(w1_raw[:], w1.rearrange("(p j) c -> p j c", j=PACK))
        nc.sync.dma_start(xw_sb[:].bitcast(I32), x_words[0].rearrange("p n t -> p (n t)").bitcast(I32))
        nc.sync.dma_start(p1_sb[:], p1)
        nc.sync.dma_start(gate[:, 0, :], ga)
        nc.sync.dma_start(p2_sb[:], p2)
        nc.sync.dma_start(gate[:, 1, :], gb)
        for a, words in enumerate((w2_words, w3_words, w4_words)):
            nc.sync.dma_start(w_words[a][:].bitcast(I32), words[0].bitcast(I32))
        for a, scale_rows in enumerate((w2_scales, w3_scales, w4_scales)):
            nc.gpsimd.memset(w_scales[a][:].bitcast(I32), 0)
            load_scale_rows(w_scales[a], scale_rows)
        for t in range(PACK):
            nc.vector.memset(neg_y[t][:, S:], 0.0)
        make_identity(nc, ident[:])

        def quantize(name, values, width):
            codes = keep.tile([P, width], U32, name=name + "_codes", align_bytes=64)
            scales = keep.tile([P, width], U8, name=name + "_scales", align_bytes=64)
            nc.vector.quantize_mx(out=codes[:].bitcast(FP8X4), scales=scales[:], in_=values)
            return codes, scales

        xs_pick = keep.tile([P, S], U8, name="xs_pick", align_bytes=64)
        nc.vector.tensor_copy(xs_pick[:], xs_sb[:].indirect(offs_sb[:]))
        w1_bf = keep.tile([P, PACK * H], BF16, name="w1_bf", align_bytes=64)
        w1_dst = w1_bf[:].rearrange("p (t m j) -> p m t j", t=PACK, j=PACK)
        w1_src = w1_raw[:].rearrange("p j (m t) -> p m t j", t=PACK)
        nc.vector.tensor_copy(w1_dst[:, :W1_ON_VECTOR], w1_src[:, :W1_ON_VECTOR])
        nc.scalar.copy(w1_dst[:, W1_ON_VECTOR:], w1_src[:, W1_ON_VECTOR:])
        w1_codes, w1_scales = quantize("w1", w1_bf[:], H)
        xw_pick = []
        for u in range(2):
            words_half = keep.tile([P, 2 * P], U32, name="xw_pick%d" % u, align_bytes=64)
            entries = slice(u * 2 * P // LANES, (u + 1) * 2 * P // LANES)
            nc.vector.tensor_copy(words_half[:], xw_sb[:].indirect(offs_sb[:, entries]))
            xw_pick.append(words_half)

        y_banks = [psum.tile([P, PACK, P], F32, name="y_bank%d" % c, tag="block%d" % c) for c in range(BLOCKS)]

        def project(t, c):
            nc.tensor.matmul_mx(out=y_banks[c][:, t, :], lhsT=w1_codes[:, blocks[t]].bitcast(FP8X4),
                                lhsT_scale=w1_scales[:, blocks[t]],
                                rhs=xw_pick[c // 2][:, blocks[c % 2]].bitcast(FP8X4), rhs_scale=xs_pick[:, blocks[c]],
                                start=True, stop=True)

        for c, block in enumerate(blocks):
            project(0, c)
            if c == LAST:
                nc.vector.tensor_scalar_mul(neg_y[0][:, block], y_banks[c][:, 0, :], -1.0)
            else:
                nc.scalar.mul(neg_y[0][:, block], y_banks[c][:, 0, :], -1.0)
        for c in range(BLOCKS):
            for t in range(1, PACK):
                project(t, c)
        for t in range(1, PACK):
            for c, block in enumerate(blocks):
                nc.scalar.mul(neg_y[t][:, block], y_banks[c][:, t, :], -1.0)
        y_bf = keep.tile([P, S, PACK], BF16, name="y_bf", align_bytes=64)
        for c, block in enumerate(blocks):
            nc.scalar.copy(y_bf[:, block, :], y_banks[c][:].rearrange("p t j -> p j t"))

        def add_turned(bank, terms):
            for i, (quarter, term) in enumerate(terms):
                nc.tensor.matmul(bank[:, quarter, :], lhsT=term, rhs=ident[:], is_transpose=True,
                                 start=(i == 0), stop=(i == len(terms) - 1))

        def sort_pairs(copy, name, by_node):
            in_pairs = ring.tile([P, PACK * P], BF16, name=name, align_bytes=64)
            copy(in_pairs[:].rearrange("j (u p e) -> j u p e", u=2, e=2), by_node.rearrange("j (u e) p -> j u p e", u=2))
            return in_pairs

        def turn_pairs(copy, in_pairs, dst, tag):
            pairs = psum.tile([P, 2, P], F32, name="pairs", tag=tag)
            for u in range(2):
                nc.tensor.transpose(pairs[:, u, :], in_pairs[:].bitcast(F32)[:, blocks[u]], ident[:])
            copy(dst.bitcast(F32).rearrange("p (j u) -> p j u", u=2), pairs[:].rearrange("p u j -> p j u"))

        h_banks = [psum.tile([P, PACK, P], F32, name="h_bank%d" % c, tag="block%d" % c) for c in range(BLOCKS)]
        for t in range(PACK):
            y_by_p1 = ring.tile([P, S], F32, name="y_by_p1", align_bytes=64)
            y_by_p2 = ring.tile([P, S], F32, name="y_by_p2", align_bytes=64)
            nc.vector.tensor_tensor(y_by_p1[:], neg_y[t][:].indirect(p1_sb[:]), gate[:, 0, :], MULT)
            nc.vector.tensor_tensor(y_by_p2[:], neg_y[t][:].indirect(p2_sb[:]), gate[:, 1, :], MULT)
            neg_h_nodes = psum.tile([P, BLOCKS, P], F32, name="neg_h_nodes", tag="sum%d" % (t % 2))
            add_turned(neg_h_nodes, [(c, term[:, block]) for term in (y_by_p1, y_by_p2) for c, block in enumerate(blocks)])
            h_nodes = ring.tile([P, BLOCKS, P], F32, name="h_nodes", align_bytes=64)
            nc.scalar.mul(h_nodes[:], neg_h_nodes[:], -1.0)
            for c, block in enumerate(blocks):
                nc.tensor.transpose(h_banks[c][:, t, :], h_nodes[:, c, :], ident[:])
                nc.scalar.mul(two_h[t][:, block], h_banks[c][:, t, :], 2.0)
        h_bf = keep.tile([P, S, PACK], BF16, name="h_bf", tag="after_h", align_bytes=64)
        for c, block in enumerate(blocks):
            nc.scalar.copy(h_bf[:, block, :], h_banks[c][:].rearrange("p t j -> p j t"))

        y_codes, y_scales = quantize("y", y_bf[:].rearrange("p j t -> p (j t)"), S)

        def look_up_h(by_p1, by_p2, t, j0, width):
            entries = slice(j0 // LANES, (j0 + width) // LANES)
            for a, (dst, lists) in enumerate(((by_p1, p1_sb), (by_p2, p2_sb))):
                nc.vector.tensor_tensor(dst, two_h[t][:].indirect(lists[:, entries]), gate[:, a, j0 : j0 + width], MULT)

        def z_on_tensor(c, looked_up):
            z_nodes = psum.tile([P, PACK, P], F32, name="z_nodes", tag="sum%d" % c)
            terms = [(t, neg_y[t][:, blocks[c]]) for t in range(PACK)]
            terms.extend((t, looked_up[t][:, a, blocks[c]]) for t in range(PACK) for a in range(2))
            add_turned(z_nodes, terms)
            in_pairs = sort_pairs(nc.scalar.copy, "z_pairs", z_nodes[:])
            z_bf = keep.tile([P, PACK * P], BF16, name="z_bf%d" % c, align_bytes=64)
            turn_pairs(nc.scalar.copy, in_pairs, z_bf[:], "block%d" % c)
            return z_bf

        def z_row_on_vector(c, t, by_p1, by_p2, partial):
            look_up_h(by_p1, by_p2[:, t, :], t, c * P, P)
            nc.vector.tensor_tensor(partial[:, t, :], by_p1, neg_y[t][:, blocks[c]], ADD)

        def z_sum_on_vector(c, by_p2, partial):
            z_bf = keep.tile([P, PACK * P], BF16, name="z_bf%d" % c, align_bytes=64)
            nc.vector.tensor_tensor(z_bf[:].rearrange("p (g i t) -> p g t i", i=RUN, t=PACK),
                                    partial[:].rearrange("p t (g i) -> p g t i", i=RUN),
                                    by_p2.rearrange("p t (g i) -> p g t i", i=RUN), ADD)
            return z_bf

        def product(a, codes, scales, bank, start=False, stop=False):
            nc.tensor.matmul_mx(out=bank[:], lhsT=codes.bitcast(FP8X4), lhsT_scale=scales,
                                rhs=w_words[a][:].bitcast(FP4X4), rhs_scale=w_scales[a][:], start=start, stop=stop)

        def close_group(c, z_bf, bank):
            z_codes, z_scales = quantize("z%d" % c, z_bf[:], P)
            product(2, z_codes[:], z_scales[:], bank, stop=True)

        out_rows = out_0.rearrange("(p t) j -> p t j", t=PACK)
        out_words = out_1[0].rearrange("p n t -> p (n t)").bitcast(I32)

        def turn_out(c, bank, tag):
            o_nodes = ring.tile([P, PACK, P], F32, name="o_nodes", align_bytes=64)
            nc.scalar.copy(o_nodes[:], bank[:].rearrange("j (p t) -> j t p", t=PACK))
            back = psum.tile([P, PACK, P], F32, name="back", tag=tag)
            for t in range(PACK):
                nc.tensor.transpose(back[:, t, :], o_nodes[:, t, :], ident[:])
            o_bf = ring.tile([P, PACK * P], BF16, name="o_bf", align_bytes=64)
            nc.scalar.copy(o_bf[:].rearrange("p (j t) -> p j t", t=PACK), back[:].rearrange("p t j -> p j t"))
            o_f32 = ring.tile([P, PACK, P], F32, name="o_f32", align_bytes=64)
            nc.scalar.copy(o_f32[:], back[:])
            nc.sync.dma_start(out_rows[:, :, blocks[c]], o_f32[:])
            return o_bf

        def turn_out_last(bank):
            o_nodes = ring.tile([P, PACK, P], F32, name="o_nodes", align_bytes=64)
            nc.vector.tensor_copy(o_nodes[:], bank[:].rearrange("j (p t) -> j t p", t=PACK))
            in_pairs = sort_pairs(nc.vector.tensor_copy, "o_pairs", o_nodes[:])
            o_bf = ring.tile([P, PACK * P], BF16, name="o_bf", align_bytes=64)
            for u, tag in enumerate(("turn1", "sum1")):
                half_back = psum.tile([P, 2, P], F32, name="half_back", tag=tag)
                for e in range(2):
                    nc.tensor.transpose(half_back[:, e, :], o_nodes[:, 2 * u + e, :], ident[:])
                o_half = ring.tile([P, 2, P], F32, name="o_half", align_bytes=64)
                nc.scalar.copy(o_half[:], half_back[:])
                nc.sync.dma_start(out_rows[:, 2 * u : 2 * u + 2, blocks[LAST]], o_half[:])
                if u == 0:
                    turn_pairs(nc.vector.tensor_copy, in_pairs, o_bf[:], "sum0")
            return o_bf

        looked_up = []
        for t in range(PACK):
            both = keep.tile([P, 2, ON_TENSOR * P], F32, name="looked_up%d" % t, align_bytes=64)
            look_up_h(both[:, 0, :], both[:, 1, :], t, 0, ON_TENSOR * P)
            looked_up.append(both)
        z_rounded = [z_on_tensor(c, looked_up) for c in range(ON_TENSOR)]
        out_banks = [psum.tile([P, N], F32, name="out_bank%d" % c, tag="block%d" % c) for c in range(LAST)]
        for c in range(LAST):
            product(0, y_codes[:, blocks[c]], y_scales[:, blocks[c]], out_banks[c], start=True)

        mid = ON_TENSOR
        mid_p1_row0 = keep.tile([P, P], F32, name="mid_p1_row0", align_bytes=64)
        mid_by_p2 = keep.tile([P, PACK, P], F32, name="mid_by_p2", align_bytes=64)
        mid_partial = keep.tile([P, PACK, P], F32, name="mid_partial", align_bytes=64)
        z_row_on_vector(mid, 0, mid_p1_row0[:], mid_by_p2, mid_partial)
        h_codes, h_scales = quantize("h", h_bf[:].rearrange("p j t -> p (j t)"), S)
        mid_p1_rest = keep.tile([P, PACK - 1, P], F32, name="mid_p1_rest", tag="after_h", align_bytes=64)
        for t in range(1, PACK):
            z_row_on_vector(mid, t, mid_p1_rest[:, t - 1, :], mid_by_p2, mid_partial)
        z_rounded.append(z_sum_on_vector(mid, mid_by_p2[:], mid_partial))

        o_rounded = []
        for c, tag in enumerate(("turn1", "sum1", "turn0")):
            product(1, h_codes[:, blocks[c]], h_scales[:, blocks[c]], out_banks[c])
            close_group(c, z_rounded[c], out_banks[c])
            o_rounded.append(turn_out(c, out_banks[c], tag))

        last_bank = psum.tile([P, N], F32, name="last_bank", tag="block%d" % mid)
        product(0, y_codes[:, blocks[LAST]], y_scales[:, blocks[LAST]], last_bank, start=True)
        product(1, h_codes[:, blocks[LAST]], h_scales[:, blocks[LAST]], last_bank)
        last_both = keep.tile([P, 2, PACK, P], F32, name="last_both", tag="after_h", align_bytes=64)
        last_partial = keep.tile([P, PACK, P], F32, name="last_partial", tag="after_z", align_bytes=64)
        for t in range(PACK):
            z_row_on_vector(LAST, t, last_both[:, 0, t, :], last_both[:, 1], last_partial)
        close_group(LAST, z_sum_on_vector(LAST, last_both[:, 1], last_partial), last_bank)

        o_codes = keep.tile([P, S], U32, name="o_codes", tag="after_z", align_bytes=64)
        o_scales = keep.tile([P, S], U8, name="o_scales", align_bytes=64)

        def hand_on(c, o_bf):
            nc.vector.quantize_mx(out=o_codes[:, blocks[c]].bitcast(FP8X4), scales=o_scales[:, blocks[c]], in_=o_bf[:])
            nc.sync.dma_start(out_words[:, blocks[c]], o_codes[:, blocks[c]].bitcast(I32))

        for c, o_bf in enumerate(o_rounded):
            hand_on(c, o_bf)
        hand_on(LAST, turn_out_last(last_bank))
        for q in range(QUADRANTS):
            queue = nc.sync if q % 2 == 0 else nc.scalar
            queue.dma_start(out_2[0, 4 * q : 4 * q + 4, :].bitcast(I32), o_scales[32 * q : 32 * q + 4, :].bitcast(I32))
